import numpy as np, ml_dtypes
CORES = [24,25,26,27,28,29,30,31]
N = 8
BF = ml_dtypes.bfloat16
CA, LV, NS, RO, HA, HB = 8, 512, 5, 2, 3, 5
W, KC = CA * LV, LV // 4
K = CA * KC
def water(rng, m=16):
    z = np.linspace(1.5, -1.5, LV); res = []
    for sg in (1.0, -1.0):
        v = sg * rng.uniform(0.5, 1.5, (N, 8, 1, CA, 1)) * z + 0.5 * rng.standard_normal((N, 8, 1, CA, 1))
        v = v.astype(np.float32) + 0.25 * rng.standard_normal((N, 8, 1, CA, LV), dtype=np.float32)
        res.append(v + 0.35 * rng.standard_normal((N, 8, m, CA, LV), dtype=np.float32))
    return res
def coef(rng, m=16):
    return np.stack([rng.uniform(0.5, 1.5, (N, 8, m)), rng.uniform(2.0 ** -13, 2.0 ** -11, (N, 8, m)), rng.uniform(0.5, 1.5, (N, 8, m))], axis=-1)
def pack(te, sa, co, cu):
    return {"te": np.ascontiguousarray(te.reshape(N, 128, W)).astype(BF), "sa": np.ascontiguousarray(sa.reshape(N, 128, W)).astype(BF),
            "co": np.ascontiguousarray(co.reshape(N, 128, 3)).astype(np.float32), "cu": np.ascontiguousarray(cu.reshape(N, 8, W)).astype(np.int32)}
def setup_inputs(rng):
    te, sa = water(rng)
    return pack(te, sa, coef(rng), rng.integers(0, CA, (N, 8, W)))
def setup_inputs_spread(rng):
    te, sa = water(rng); k = (N, 8, 1, CA, LV)
    te = te * np.exp2(rng.integers(-3, 4, k)) * (rng.random(k) > 0.0625); sa = sa * np.exp2(rng.integers(-3, 4, k)) * (rng.random(k) > 0.0625)
    co = np.stack([np.exp2(rng.uniform(-2, 2, (N, 8, 16))), rng.uniform(2.0 ** -20, 2.0 ** -10, (N, 8, 16)), np.exp2(rng.uniform(-2, 2, (N, 8, 16)))], axis=-1)
    cu = np.minimum((CA * rng.random((N, 8, W)) ** 3).astype(np.int64), CA - 1)
    return pack(te, sa, co, cu)
def setup_inputs_ends(rng):
    b = 4096.0; pt = np.ones((8, CA, LV)); ps = np.ones((8, CA, LV)); pc = np.zeros((8, CA, LV), np.int64)
    pt[:, 0] = -1; ps[:, 0] = -1; pc[:, 0] = CA - 1
    for c in range(1, CA - 1):
        if c % 4 == 3: ps[:, c] = -1; pt[:, c, :2] = -1; ps[:, c, :2] = 1; pc[:, c] = CA - 1
        else: pt[:, c] = -1; pt[:, c, LV - 2:] = 1; ps[:, c, LV - 2:] = -1
    pt[1::2, CA - 1, LV - 4] = -1; ps[1::2, CA - 1, LV - 2:] = -1
    def turned(m, share, col):
        t = (rng.random((N, 8, m, CA, LV), dtype=np.float32) < share) ^ (rng.random((N, 8, 1, CA, LV), dtype=np.float32) < col)
        t[..., :8] = False; t[..., LV - 8:] = False; t[:, :, :, 0] = False; t[:, :, :, CA - 1] = False
        return t
    te = np.where(turned(16, 0.15, 0.1), -b, b).astype(np.float32) * pt[None, :, None].astype(np.float32)
    sa = np.where(turned(16, 0.15, 0.1), -b, b).astype(np.float32) * ps[None, :, None].astype(np.float32)
    n = te[:, :, :, 4:CA - 1:4].shape
    te[:, :, :, 4:CA - 1:4] = rng.uniform(-b, b, n); sa[:, :, :, 4:CA - 1:4] = rng.uniform(-b, b, n)
    cu = np.where(turned(1, 0.2, 0.0)[:, :, 0], CA - 1 - pc[None], pc[None])
    cu[:, :, 4:CA - 1:4] = (CA - 1) * rng.integers(0, 2, cu[:, :, 4:CA - 1:4].shape)
    good = np.argsort(rng.random((N, 8, 16)), axis=-1) < 11
    co = np.stack([np.where(good | (rng.random((N, 8, 16)) < 0.5), 4.0, 0.25), np.where(rng.random((N, 8, 16)) < 0.5, 0.0, 2.0 ** -10), np.where(good | (rng.random((N, 8, 16)) < 0.5), 0.25, 4.0)], axis=-1)
    return pack(te, sa, co, cu)
def setup_inputs_corners(rng):
    te, sa = water(rng); te = te + rng.choice(np.array([-3.0, 0.0, 3.0]), (N, 8, 1, 1, 1))
    own = np.repeat(np.arange(CA), LV); lev = np.arange(W) % LV; cu = rng.integers(0, CA, (N, 8, W)); any3 = rng.integers(0, 3, (N, 8, W))
    for r in range(N):
        for g in range(8):
            k = (r + g) % 8
            if k == 0: cu[r, g] = own
            elif k == 1: cu[r, g] = 0
            elif k == 2: cu[r, g] = CA - 1
            elif k == 3: cu[r, g] = (own + 1) % CA
            elif k == 4: cu[r, g] = CA - 1 - own
            elif k == 5: cu[r, g] = np.where((lev >> 2) % 2 == 0, 0, CA - 1)
            elif k == 6: cu[r, g] = np.where(any3[r, g] == 0, 0, np.where(any3[r, g] == 1, CA - 1, own))
    co = coef(rng); h = CA // 2
    te[:, 2::4, :, :h] = 0; te[:, 2::4, :, h:] = 1; sa[:, 2::4, :, :h] = 0; sa[:, 2::4, :, h:] = 1
    for r in range(N):
        for g in (2, 6):
            x0 = 128 * (KC // 4 + 1 + 2 * int(rng.integers(0, KC // 8)))
            a0 = rng.uniform(0.5, 1.5, 4096).astype(np.float32); a1 = (rng.uniform(0.5, 1.0, 4096) / x0).astype(np.float32)
            two = a1 * np.float32(x0) + a0; one = (a1.astype(np.float64) * x0 + a0.astype(np.float64)).astype(np.float32)
            k = np.argsort(np.where(one > two, 0, 1), kind="stable")[:16]
            co[r, g] = np.stack([a0[k], a1[k], two[k]], axis=-1); cu[r, g] = rng.integers(h, CA, W)
    f4 = np.float32
    for r in range(N):
        ra = (r + HA) % N; rb = (r + HB) % N
        for g in (1, 3, 4, 5, 7):
            j = KC // 4 + 1 + int(rng.integers(0, KC // 4)); l = 4 * j + 1; x0 = 128 * j + (28 if g == 4 else 24)
            a0 = rng.uniform(0.5, 1.5, 4096).astype(f4); a1 = (rng.uniform(0.5, 1.0, 4096) / x0).astype(f4); w = a1 * f4(x0) + a0
            tu = np.full(4096, 32, f4); su = np.full(4096, 32, f4); b0 = np.nextafter(w, f4(0)); ok = np.ones(4096, bool)
            if g == 1:
                b0 = w; ok = ((a1 * f4(x0 - 8) + a0) + a1 * f4(8)) > w
            if g in (3, 7):
                tu = (2 * rng.integers(64, 128, 4096)).astype(f4); su = (2 * rng.integers(64, 128, 4096)).astype(f4)
                left = tu * w; b0 = left / su; ok = (su * b0 == left) & (b0 < 4)
                if g == 3: ok = ok & (tu.astype(np.float64) * w.astype(np.float64) > su.astype(np.float64) * b0.astype(np.float64))
                else: ok = ok & (left * (f4(1) / b0) > su)
                b0 = np.minimum(b0, f4(4))
            k = np.argsort(np.where(ok, 0, 1), kind="stable")[:16]
            tl, tr = (2816, -1280) if g == 4 else (1792, -2304)
            sl, sr, s1 = 0.0, 0.0, -su[k]
            if g == 4: sl, sr, s1 = 1.25 * 2.0 ** -18, -128.0, np.full(16, -128.0)
            if g == 5: sl, sr, s1 = -224.0, 288.0, np.full(16, -2.0 ** -18)
            te[ra, g, :, 1, :l + 1] = tl; te[ra, g, :, 1, l + 1:] = tr
            sa[ra, g, :, 1, :l + 1] = sl; sa[ra, g, :, 1, l + 1:] = sr
            te[r, g, :, 4:, 4 * j] = (-256 - tu[k])[:, None]; sa[r, g, :, 4:, 4 * j] = s1[:, None]
            cu[r, g, 4 * LV + 4 * j::LV] = 1; cu[ra, g, LV + l] = int(rng.integers(4, CA))
            co[ra, g] = np.stack([a0[k], a1[k], b0[k]], axis=-1)
        te[r, 7, :, 4:, LV - 4] = -544; sa[r, 7, :, 4:, LV - 4] = -32; cu[r, 7, 5 * LV - 4::LV] = 2
        te[ra, 7, :, 2] = -288; sa[ra, 7, :, 2] = -32; cu[ra, 7, 3 * LV - 2] = 3
        te[rb, 0, :, 3, LV - 2] = 3328; te[rb, 0, :, 3, LV - 1] = -768; sa[rb, 0, :, 3, LV - 2:] = 0
        xm = 32 * (LV - 2) + 28
        a0 = rng.uniform(0.5, 1.5, 16).astype(f4); a1 = (rng.uniform(0.5, 1.0, 16) / xm).astype(f4)
        co[rb, 0] = np.stack([a0, a1, a1 * f4(xm - 1) + a0], axis=-1)
    return pack(te, sa, co, cu)
def setup_inputs_crowd(rng):
    te, sa = water(rng, 1); e = rng.permutation(16); sg = np.ones((8, 16), np.float32)
    for g in range(8): sg[g, e[:(0, 1, 7, 8)[g % 4]]] = -1
    te = te * sg[None, :, :, None, None]; sa = sa * sg[None, :, :, None, None]
    co = np.repeat(coef(rng, 1), 16, axis=2)
    one = rng.integers(0, CA, (N, 8)); cu = np.repeat(one[:, :, None], W, axis=2)
    for r in range(N):
        for g in range(1, 8, 2): cu[r, g, 4 * int(rng.integers(0, K))] = (one[r, g] + 1 + int(rng.integers(0, CA - 1))) % CA
    return pack(te, sa, co, cu)
def setup_inputs_calm(rng):
    te, sa = water(rng); co = coef(rng); cu = rng.integers(0, CA, (N, 8, CA, LV))
    e = rng.permutation(16); up = np.zeros(16, bool); up[e[:8]] = True
    t = 0.25 * rng.integers(-4, 5, 16); s = 0.25 * rng.integers(-4, 5, 16)
    sa[:, :, :, :4] = s[None, None, :, None, None]; sa[:, :, :, :, :2] = s[None, None, :, None, None]; sa[:, :, :, :, LV - 4:] = s[None, None, :, None, None]
    te[:, :, :, :4] = t[None, None, :, None, None]; te[:, :, :, 3] += 1; te[:, :, int(e[0]), 0] += 0.9
    for g in range(4):
        a1 = t + 1 - 16 / (2 * g + 1); b1 = t - 1 + 16 / (1.0, 1.0, 1.5, 1.8)[g]
        te[:, g, :, 4:, 0] = np.where(up, t + 1, t - 1)[None, :, None]; te[:, g, :, 4:, 1] = np.where(up, a1, b1)[None, :, None]
    for g in range(4, 8):
        for lv, v in ((LV - 4, -1.0), (LV - 3, -1.3684), (LV - 2, 2.0), (LV - 1, 2.0 if g % 2 == 0 else 2 - 16 / 13)): te[:, g, :, 4:, lv] = (t + v)[None, :, None]
    cu[:, :4, 4:, :4] = 0; cu[:, 4:, 4:, LV - 4:] = 2; cu[:, :, 0] = 1; cu[:, :, 2] = 3
    cu[:, :, 0, 8:] = rng.integers(4, CA, (N, 8, LV - 8))
    return pack(te, sa, co, cu)
def check_inputs(d):
    bad = []
    if np.min(d["cu"]) < 0 or np.max(d["cu"]) > CA - 1: bad.append("range of cu")
    for k in ("te", "sa"):
        a = np.abs(np.asarray(d[k]).astype(np.float32))
        if not np.max(a) <= 4096: bad.append("range of " + k)
        if np.any((a > 0) & (a < 2.0 ** -60)): bad.append("least size in " + k)
    c = np.asarray(d["co"]).astype(np.float64)
    for j, lo, hi in ((0, 0.25, 4.0), (1, 0.0, 2.0 ** -10), (2, 0.25, 4.0)):
        if not (np.min(c[..., j]) >= lo and np.max(c[..., j]) <= hi): bad.append("range of co, column " + str(j))
    if np.any((c[..., 1] > 0) & (c[..., 1] < 2.0 ** -20)): bad.append("least size in co, column 1")
    return bad
def reference(te, sa, co, cu):
    tw = te.astype(np.float32).reshape(N, 8, 16, W); sw = sa.astype(np.float32).reshape(N, 8, 16, W)
    cf = co.astype(np.float32).reshape(N, 8, 16, 3); cr = cu.astype(np.int64)
    base = (np.arange(N * 128) * W).reshape(N, 8, 16, 1); cbase = (np.arange(N * 8) * W).reshape(N, 8, 1)
    def pick(a, at):
        return np.take(a.reshape(-1), base + at[:, :, None, :])
    def moved(a, o, sh):
        return np.roll(a, (-o, -sh), (0, 1))
    def frac(k):
        return k.astype(np.float32)[:, :, None, :] * np.float32(0.0625)
    def passed(tv, sv, t1, s1, x, c):
        w = c[..., 1:2] * x.astype(np.float32)[:, :, None, :] + c[..., 0:1]
        yes = (tv - t1) * w > (sv - s1) * c[..., 2:3]
        return np.add.reduce(yes.astype(np.int64), axis=2) >= 9
    home = np.ascontiguousarray(np.broadcast_to(np.arange(K) // KC, (N, 8, K)))
    dep = np.ascontiguousarray(np.broadcast_to(64 * (np.arange(K) % KC), (N, 8, K)))
    for rnd in range(RO):
        d = dep; c = home; col = c * LV + (d >> 4); k = frac(d & 15)
        lo = pick(tw, col); t1 = lo + (pick(tw, col + 1) - lo) * k
        lo = pick(sw, col); s1 = lo + (pick(sw, col + 1) - lo) * k
        cnow = cr
        for hop, (o, sh) in enumerate(((HA, 0), (HB, 1), (0, 0))):
            c = np.take(cnow.reshape(-1), cbase + c * LV + (d >> 4)) if hop < 2 else home
            cnow = moved(cr, o, sh); th = moved(tw, o, sh); sh_ = moved(sw, o, sh); ch = moved(cf, o, sh)
            l = d >> 4
            for j in range(NS - 1, -1, -1):
                st = 2 ** j
                ok = passed(pick(th, c * LV + l), pick(sh_, c * LV + l), t1, s1, d + 16 * l, ch)
                l = np.where(ok, np.minimum(l + st, LV - 2), np.maximum(l - st, 0))
            ta = pick(th, c * LV + l); tb = pick(th, c * LV + l + 1) - ta
            sa_ = pick(sh_, c * LV + l); sb = pick(sh_, c * LV + l + 1) - sa_
            q = np.zeros_like(l)
            for h in (8, 4, 2):
                k = frac(q + h)
                ok = passed(ta + tb * k, sa_ + sb * k, t1, s1, d + 16 * l + q + h, ch)
                q = np.where(ok, q + h, q)
            k = frac(q); t1 = ta + tb * k; s1 = sa_ + sb * k; d = 16 * l + q
        dep = dep + ((d - dep) >> 1)
        old = tw[..., rnd::4]; tw[..., rnd::4] = old + (t1 - old) * np.float32(0.25)
        old = sw[..., rnd::4]; sw[..., rnd::4] = old + (s1 - old) * np.float32(0.25)
    return {"yt": np.ascontiguousarray(tw[..., RO - 1::4]).reshape(N, 128, K), "ys": np.ascontiguousarray(sw[..., RO - 1::4]).reshape(N, 128, K), "yd": dep.astype(np.float32)}

@@ -1,0 +1,555 @@
+from concourse.mybir import AluOpType, ActivationFunctionType
+
+N = 8
+HA, HB = 3, 5
+NC = 4
+CH = 256
+W = 4096
+CW = W // NC
+
+SCRATCH = {
+    "HT": ("sbuf", [128, W], "bfloat16"), "HS": ("sbuf", [128, W], "bfloat16"),
+    "AT": ("sbuf", [128, W], "bfloat16"), "AS": ("sbuf", [128, W], "bfloat16"),
+    "hT": ("sbuf", [128, W], "float32"), "hS": ("sbuf", [128, W], "float32"),
+    "aT": ("sbuf", [128, W], "float32"), "aS": ("sbuf", [128, W], "float32"),
+    "bT": ("sbuf", [128, W], "float32"), "bS": ("sbuf", [128, W], "float32"),
+    "cuT": ("sbuf", [128, W], "bfloat16"),
+    "cui": ("sbuf", [128, 256], "int32"), "cc": ("sbuf", [128, 256], "bfloat16"), "ccA": ("sbuf", [128, 256], "bfloat16"),
+    "coH": ("sbuf", [128, 4], "float32"), "coA": ("sbuf", [128, 4], "float32"), "coB": ("sbuf", [128, 4], "float32"),
+    "U": ("sbuf", [128, 2048], "float32"), "L1": ("sbuf", [128, 2048], "float32"),
+    "dBT": ("dram", [128, W], "bfloat16"), "dBS": ("dram", [128, W], "bfloat16"),
+    "dco": ("dram", [128, 3], "float32"), "dU": ("dram", [128, 2048], "float32"),
+    "pid": ("sbuf", [128, 4], "int32"), "dif": ("sbuf", [128, 128], "float32"), "rel": ("sbuf", [128, 128], "float32"),
+    "BD": ("sbuf", [128, 128], "float32"), "tmp": ("sbuf", [128, 128], "float32"),
+    "cf": ("sbuf", [128, 24], "float32"), "colm": ("sbuf", [128, 16], "float32"), "cold": ("sbuf", [128, 16], "float32"),
+    "cq": ("sbuf", [128, 4], "float32"),
+    "i0": ("sbuf", [128, 64], "float32"), "i1": ("sbuf", [128, 64], "float32"), "i2": ("sbuf", [128, 16], "float32"),
+    "MH": ("sbuf", [128, 17 * 128], "float16"),
+    "MB": ("sbuf", [128, 28 * 128], "bfloat16"),
+    "L0": ("sbuf", [128, 64], "float16"), "HC": ("sbuf", [128, 64], "float16"), "JJ": ("sbuf", [128, 16], "float16"),
+    "M8": ("sbuf", [128, 64], "bfloat16"),
+}
+for _h in range(NC):
+    SCRATCH["W%d" % _h] = ("sbuf", [128, 14 * CH], "float32")
+    SCRATCH["B%d" % _h] = ("sbuf", [128, 2 * CH + 7 * 64], "bfloat16")
+    SCRATCH["H%d" % _h] = ("sbuf", [128, 3 * 64], "float16")
+    SCRATCH["I%d" % _h] = ("sbuf", [128, 2 * 64], "int32")
+    SCRATCH["O%d" % _h] = ("sbuf", [128, 3 * 16], "uint16")
+    SCRATCH["P%d" % _h] = ("psum", [128, 2 * CH], "float32")
+    SCRATCH["Q%d" % _h] = ("psum", [128, 2 * CH], "float32")
+
+SEMAPHORES = ["V", "S", "P", "G"] + ["d%d" % _k for _k in range(40)] + ["l%d" % _k for _k in range(14)] + ["r%d" % _k for _k in range(14)]
+
+EST = {"cyc": 0.83, "gat": 1.56, "pe": 0.42, "lat": 160.0, "bw": 300.0, "lead": 1.5, "pw": 1.0, "look": 0.0}
+BOTH_ON_SCALAR = ()
+
+
+def cost_ns(c, e):
+    k, n = c
+    if k == "1": return max(64, n) * e["cyc"]
+    if k == "h": return max(64, n / 2) * e["cyc"]
+    if k == "2": return max(64, 2 * n) * e["cyc"]
+    if k == "g": return 65 + n * e["gat"] * e["cyc"]
+    if k == "t": return 50 + n * e.get("tt", e["gat"]) * e["cyc"]
+    if k == "pe": return n * e["pe"]
+    return n
+
+
+def plan(g, T, topo, core):
+    A = AluOpType
+    F = ActivationFunctionType
+    rank = T.rank_of(core)
+    ops = []
+    last, readers, banks = {}, {}, {}
+    cnt = {"d": 0, "r": 0, "h": 0}
+    step = [0] * NC
+    bank_of = {"pT": "P", "pB": "P", "pS": "Q", "pC": "Q"}
+
+    def op(eng, cost, reads, writes, fn, kind="c", after=(), nbytes=0, sem=None, val=0):
+        i = len(ops)
+        deps = set(after)
+        for r in reads:
+            if r in last: deps.add(last[r])
+        for w in writes:
+            if w in last: deps.add(last[w])
+            deps.update(readers.get(w, ()))
+        for bk in set(bank_of[x[:2]] + x[2:] for x in reads + writes if x[:2] in bank_of):
+            who, now, before = banks.get(bk, (eng, [], []))
+            if who != eng: now, before = [], now
+            deps.update(before)
+            banks[bk] = (eng, now + [i], before)
+        for r in reads: readers.setdefault(r, []).append(i)
+        for w in writes:
+            last[w] = i
+            readers[w] = []
+        deps.discard(i)
+        ops.append({"eng": eng, "cost": cost, "deps": deps, "fn": fn, "kind": kind, "bytes": nbytes, "sem": sem, "val": val, "sim": (),
+                    "h": cnt["h"], "step": step[cnt["h"]]})
+        return i
+
+    def V(cost, reads, writes, fn): return op("V", cost, reads, writes, fn)
+    def S(cost, reads, writes, fn): return op("S", cost, reads, writes, fn)
+
+    def ts(out, in0, s1, s2, o0, o1=None):
+        if o1 is None: return lambda: g.vector.tensor_scalar(out, in0, s1, None, o0)
+        return lambda: g.vector.tensor_scalar(out, in0, s1, s2, o0, o1)
+    def tt(out, a, b, o): return lambda: g.vector.tensor_tensor(out, a, b, o)
+    def cp(out, a): return lambda: g.vector.tensor_copy(out, a)
+    def act(out, a, f=None, **kw): return lambda: g.scalar.activation(out, a, F.Identity if f is None else f, **kw)
+
+    def PE(reads, writes, groups, onto=False, cycles=None, one=False):
+        def fn():
+            ins = None
+            for x, (out, terms) in enumerate(groups):
+                for k, (l, r) in enumerate(terms):
+                    ins = g.tensor.matmul(out, l, r, k == 0 and not onto and not (one and x),
+                                          k == len(terms) - 1 and not one)
+            return ins
+        return op("P", ("pe", cycles or 64 * sum(len(t) for _, t in groups)), reads, writes, fn)
+
+    def dma(q, reads, writes, out, in_, nbytes, after=()):
+        sem = "d%d" % cnt["d"]
+        cnt["d"] += 1
+        e = g if q == "G" else g.sync
+        return op(q, ("n", 1000.0 if q == "G" else 100.0), reads, writes, lambda: e.dma_start(out, in_), "dma", after, nbytes, sem, 16)
+
+    def send(away, reads, writes, out, in_, nbytes, after=()):
+        k = cnt["r"]
+        cnt["r"] += 1
+        dst = T.cores[(rank - away) % N]
+        src = T.cores[(rank + away) % N]
+        rid, pid, _ = topo.addr(dst)
+        m = topo.mask(core, dst)
+        i = op("G", ("n", 1000.0), reads, [], lambda: g.remote_dma(out, in_, T.sem["r%d" % k], T.sem["l%d" % k], pid, rid, m),
+               "send", after, nbytes, "l%d" % k, len(topo.engines(core, dst)))
+        j = op("X", ("n", 0.0), [], writes, None, "land", (), 0, "r%d" % k, len(topo.engines(src, core)))
+        ops[j]["deps"] = set()
+        ops[j]["sim"] = (i,)
+        return i
+
+    def col(t, k): return t[:, k:k + 1]
+    def every(x): return [x + str(h) for h in range(NC)]
+
+    dma("Y", [], ["coH"], T.coH[:, 0:3], T.co[:, :], 1536)
+    dma("Y", [], ["cui"], T.cui[:, :], T.cu[:, :], 131072)
+    dma("Y", [], ["HT"], T.HT[:, :], T.te[:, :], 1 << 20)
+    dma("Y", [], ["HS"], T.HS[:, :], T.sa[:, :], 1 << 20)
+
+    def numbers(name, out, pat, cm):
+        op("G", ("n", 300.0), [], [name], lambda: g.iota(out, pat, 0, cm, allow_small_or_imprecise_dtypes=True))
+    op("G", ("n", 140.0), [], ["pid"], lambda: g.iota(T.pid[:, 0:1], [[0, 1]], 0, 1))
+    numbers("dif", T.dif[:, :], [[1, 128]], -1)
+    numbers("i0", T.i0[:, :], [[0, 2], [16, 32]], 0)
+    numbers("i1", T.i1[:, :], [[512, 2], [0, 32]], 0)
+    numbers("i2", T.i2[:, :], [[16, 16]], 0)
+
+    V(("h", W), [], ["cuT"], lambda: g.vector.memset(T.cuT[:, :], 0.0))
+    V(("1", 256), ["cui"], ["cc"], ts(T.cc[:, :], T.cui[:, :], 512.0, None, A.mult))
+    dma("Y", ["cc"], ["cuT"], T.cuT[0:128:16, :], T.cc[:, :], 65536)
+
+    send(HA, ["coH"], ["coA"], T.coA[:, 0:3], T.coH[:, 0:3], 1536)
+    s1 = send(HA, ["HT"], ["AT"], T.AT[:, :], T.HT[:, :], 1 << 20)
+    s2 = send(HA, ["HS"], ["AS"], T.AS[:, :], T.HS[:, :], 1 << 20)
+    send(HA, ["cc"], ["ccA"], T.ccA[:, :], T.cc[:, :], 65536)
+    send(HB, ["coH"], ["dco"], T.dco[:, :], T.coH[:, 0:3], 1536, (s1, s2))
+    send(HB, ["HT"], ["dBT"], T.dBT[:, :], T.HT[:, :], 1 << 20)
+    send(HB, ["HS"], ["dBS"], T.dBS[:, :], T.HS[:, :], 1 << 20)
+    for nm, dn, tab, src in (("bT", "dBT", T.bT, T.dBT), ("bS", "dBS", T.bS, T.dBS)):
+        dma("G", [dn], [nm + "x"], tab[0:112, :], src[16:128, :], 7 << 18)
+        dma("G", [dn], [nm + "y"], tab[112:128, :], src[0:16, :], 1 << 18)
+    dma("G", [], every("hT"), T.hT[:, :], T.te[:, :], 2 << 20)
+    dma("G", [], every("hS"), T.hS[:, :], T.sa[:, :], 2 << 20)
+    dma("G", ["AT"], ["aT0", "aT1"], T.aT[:, :], T.AT[:, :], 2 << 20)
+    dma("G", ["AS"], ["aS0", "aS1"], T.aS[:, :], T.AS[:, :], 2 << 20)
+
+    c1, c128 = ("1", 1), ("1", 128)
+    names = ["PIDF", "Q", "Q3", "QC", "C0", "C1", "C2", "C3", "CLIP", "QM1", "HMC", "SELW", "Q4", "LOW", "KEEP", "EVEN", "x0", "x1"]
+    C = {nm: col(T.cf, k) for k, nm in enumerate(names)}
+
+    def column(nm, src, s1, s2, o0, o1=None):
+        rd = [src] + [s for s in (s1, s2) if isinstance(s, str)]
+        V(c1, rd, [nm], ts(C[nm], C[src], C.get(s1, s1), C.get(s2, s2), o0, o1))
+    V(c1, ["pid"], ["PIDF"], cp(C["PIDF"], col(T.pid, 0)))
+    V(c1, ["pid"], ["iq"], ts(col(T.pid, 1), col(T.pid, 0), 15, None, A.bitwise_and))
+    V(c1, ["pid"], ["iq3"], ts(col(T.pid, 2), col(T.pid, 0), 3, None, A.bitwise_and))
+    V(c1, ["iq"], ["Q"], cp(C["Q"], col(T.pid, 1)))
+    V(c1, ["iq3"], ["Q3"], cp(C["Q3"], col(T.pid, 2)))
+    column("QC", "Q", "Q3", 0.25, A.subtract, A.mult)
+    for k in range(4): column("C%d" % k, "QC", float(k), None, A.is_equal)
+    column("CLIP", "C0", -3586.0, 4096.0, A.mult, A.add)
+    column("QM1", "C3", -1.0, None, A.mult)
+    column("x0", "C3", 0.5, None, A.mult)
+    column("HMC", "C2", 8.0, "x0", A.mult, A.add)
+    column("x1", "C1", 2.0 * CH / 2, None, A.mult)
+    column("SELW", "C0", CH / 2, "x1", A.mult, A.add)
+    column("Q4", "Q3", 4.0, None, A.mult)
+    column("LOW", "QC", 1.5, None, A.is_lt)
+    column("KEEP", "QC", 1.0, None, A.not_equal)
+    column("EVEN", "C0", "C2", None, A.add)
+    dif, rel, BD = T.dif[:, :], T.rel[:, :], T.BD[:, :]
+    V(c128, ["dif", "Q"], ["rel"], ts(rel, dif, C["Q"], None, A.add))
+    V(c128, ["rel"], ["tmp"], ts(T.tmp[:, :], rel, -0.5, None, A.is_gt))
+    V(c128, ["rel"], ["BD"], ts(BD, rel, 15.5, None, A.is_lt))
+    V(("2", 128), ["tmp", "BD"], ["BD"], tt(BD, BD, T.tmp[:, :], A.mult))
+    V(c1, ["dif", "PIDF", "Q"], ["colm"], ts(T.colm[:, :], T.dif[:, 0:16], C["PIDF"], C["Q"], A.add, A.is_equal))
+    V(c1, ["colm"], ["cd0"], ts(T.cold[:, 0:4], T.colm[:, 8:12], 16.0, None, A.mult))
+    V(c1, ["colm", "cd0"], ["cd"], tt(T.cold[:, 4:8], T.cold[:, 0:4], T.colm[:, 12:16], A.add))
+    V(c1, ["colm"], ["cx0"], ts(T.cold[:, 8:12], T.colm[:, 0:4], 16.0, None, A.mult))
+    V(c1, ["cd", "cx0"], ["cx"], tt(T.cold[:, 12:16], T.cold[:, 8:12], T.cold[:, 4:8], A.add))
+    V(c1, ["i2", "Q3"], ["cq"], ts(T.cq[:, :], T.i2[:, 0:4], 0.25, C["Q3"], A.mult, A.add))
+    M = {}
+    for k, nm in enumerate(["I", "KP", "E", "HM", "E0"] + every("RX") + every("RD") + every("MA")):
+        M[nm] = T.MH[:, 128 * k:128 * k + 128]
+    for k, nm in enumerate(["CN%d" % p for p in range(8)] + every("R1") + every("RK") + every("SA") + ["S16", "S8", "S4", "S2", "S1", "SH", "SY2", "SY3"]):
+        M[nm] = T.MB[:, 128 * k:128 * k + 128]
+    for p in range(8):
+        V(c128, ["rel"], ["CN%d" % p], ts(M["CN%d" % p], rel, float(p), None, A.is_equal))
+    for p in range(4):
+        x = str(p)
+        V(c128, ["BD", "cx"], ["RX" + x], ts(M["RX" + x], BD, col(T.cold, 12 + p), None, A.mult))
+        V(c128, ["BD", "cd"], ["RD" + x], ts(M["RD" + x], BD, col(T.cold, 4 + p), None, A.mult))
+        S(c128, ["BD", "colm"], ["R1" + x], act(M["R1" + x], BD, scale=col(T.colm, p)))
+        S(c128, ["R1" + x], ["RK" + x], act(M["RK" + x], M["R1" + x], scale=0.0625))
+        V(c128, ["rel", "cq", "LOW"], ["MA" + x], ts(M["MA" + x], rel, col(T.cq, p), C["LOW"], A.is_equal, A.mult))
+        V(c128, ["rel", "cq", "SELW"], ["SA" + x], ts(M["SA" + x], rel, col(T.cq, p), C["SELW"], A.is_equal, A.mult))
+    V(c128, ["dif"], ["I"], ts(M["I"], dif, 0.0, None, A.is_equal))
+    V(c128, ["dif", "KEEP"], ["KP"], ts(M["KP"], dif, 0.0, C["KEEP"], A.is_equal, A.mult))
+    V(c128, ["dif", "LOW"], ["E"], ts(M["E"], dif, 0.0, C["LOW"], A.is_equal, A.mult))
+    V(c128, ["dif", "C0"], ["E0"], ts(M["E0"], dif, 8.0, C["C0"], A.is_equal, A.mult))
+    V(("2", 128), ["E", "E0"], ["E"], tt(M["E"], M["E"], M["E0"], A.add))
+    V(c128, ["rel", "Q3", "HMC"], ["HM"], ts(M["HM"], rel, C["Q3"], C["HMC"], A.is_equal, A.mult))
+    V(c128, ["dif", "C0"], ["S1"], ts(M["S1"], dif, 0.0, C["C0"], A.is_equal, A.mult))
+    for s in (16, 8, 4, 2):
+        S(c128, ["S1"], ["S%d" % s], act(M["S%d" % s], M["S1"], scale=float(s)))
+    V(c128, ["dif", "C0"], ["SH"], ts(M["SH"], dif, 12.0, C["C0"], A.is_equal, A.mult))
+    V(c128, ["dif", "C0"], ["SY3"], ts(M["SY3"], dif, 4.0, C["C0"], A.is_equal, A.mult))
+    V(("2", 128), ["SY3", "S1"], ["SY2"], tt(M["SY2"], M["SY3"], M["S1"], A.subtract))
+    V(("2", 128), ["SY3", "S2"], ["SY3"], tt(M["SY3"], M["SY3"], M["S2"], A.add))
+    V(c1, ["i0", "Q4", "EVEN"], ["L0"], ts(T.L0[:, :], T.i0[:, :], C["Q4"], C["EVEN"], A.add, A.mult))
+    V(c1, ["i1", "C1"], ["HC"], ts(T.HC[:, :], T.i1[:, :], C["C1"], None, A.mult))
+    V(c1, ["i2", "Q"], ["JJ"], ts(T.JJ[:, :], T.i2[:, :], C["Q"], 1.5 * CH, A.add, A.add))
+    V(c1, [], ["M8"], lambda: g.vector.memset(T.M8[:, :], 8.0))
+
+    big, gat, gtt, sm = ("1", CH), ("g", CH), ("t", CH), ("1", 64)
+
+    def chunk(h):
+        cnt["h"] = h
+        x = str(h)
+        at = {}
+        for k, nm in enumerate(["WT0", "WT1", "WT2", "WT3", "WS0", "WS1", "WS2", "WS3", "tb", "sb", "T1", "dT", "dS", "gS"]):
+            at[nm] = (T["W" + x], k * CH, CH)
+        at["WT"], at["WS"] = (T["W" + x], 0, 4 * CH), (T["W" + x], 4 * CH, 4 * CH)
+        at["vo"], at["cr"] = (T["B" + x], 0, CH), (T["B" + x], CH, CH)
+        for k, nm in enumerate(["sg", "g1", "g2", "g3", "m2", "m3", "ys"]): at[nm] = (T["B" + x], 2 * CH + 64 * k, 64)
+        for k, nm in enumerate(["Z", "F", "dl"]): at[nm] = (T["H" + x], 64 * k, 64)
+        for k, nm in enumerate(["ia", "ib"]): at[nm] = (T["I" + x], 64 * k, 64)
+        for k, nm in enumerate(["of", "og", "se"]): at[nm] = (T["O" + x], 16 * k, 16)
+        at["pT"], at["pB"], at["pS"], at["pC"] = (T["P" + x], 0, CH), (T["P" + x], CH, CH), (T["Q" + x], 0, CH), (T["Q" + x], CH, CH)
+        at["U0"], at["U1"] = (T.U, 2 * CH * h, CH), (T.U, 2 * CH * h + CH, CH)
+
+        def b(nm, first=0, end=None, by=1):
+            t, o, w = at[nm]
+            if by == 1: return t[:, o + first:o + (w if end is None else end)]
+            return t[:, o + first:o + (w if end is None else end):by]
+        return b, (lambda nm: nm + x)
+
+    def spread(h, bank, parts, one=False):
+        b, n = chunk(h)
+        reads = []
+        for f, nm, _ in parts: reads += [nm] + every(f)
+        PE(reads, [n(bank)], [(b(bank, p, CH, 4), [(M[f + str(p)], t) for f, _, t in parts]) for p in range(4)], one=one)
+
+    def offsets(h, both):
+        b, n = chunk(h)
+        o = b("pC", 128, 144)
+        PE([n("Z")] + every("MA"), [n("pC")], [(o, [(M["MA%d" % a], b("Z", a, 64, 4)) for a in range(4)])])
+        V(sm, [n("pC")], [n("of")], cp(b("of"), o))
+        if both: V(sm, [n("pC")], [n("og")], ts(b("og"), o, 1.0, None, A.add))
+
+    def new_cast(h, src, terms, reads):
+        b, n = chunk(h)
+        o = b("pC", 64, 128)
+        PE(reads + ["KP"], [n("pC")], [(o, [(M["KP"], src)] + terms)])
+        V(sm, [n("pC")], [n("Z")], cp(b("Z"), o))
+
+    def count(h, sg):
+        b, n = chunk(h)
+        o = b("pC", 0, 64)
+        V(big, [n("pB"), n("dS")], [n("vo")], tt(b("vo"), b("pB"), b("dS"), A.is_gt))
+        PE([n("vo")] + every("CN"), [n("pC")], [(o, [(M["CN%d" % p], b("vo", p, CH, 4)) for p in range(4)])])
+        step[h] += 1
+        S(sm, [n("pC")], [n(sg)], act(b(sg), o, F.Sign, bias=-8.5))
+
+    def pair(h, tw, sw, tn, sn):
+        b, n = chunk(h)
+        S(gat, sn + [n("of")], [n("WS0")], act(b("WS0"), sw.indirect(b("of"))))
+        S(gat, tn + [n("of")], [n("WT0")], act(b("WT0"), tw.indirect(b("of"))))
+        V(gtt, sn + [n("og"), n("WS0")], [n("sb")], tt(b("sb"), sw.indirect(b("og")), b("WS0"), A.subtract))
+        V(gtt, tn + [n("og"), n("WT0")], [n("tb")], tt(b("tb"), tw.indirect(b("og")), b("WT0"), A.subtract))
+
+    casts = ["CN4", "CN5", "CN6", "CN7"]
+
+    def current(h, cw, row):
+        b, n = chunk(h)
+        S(gat, ["cuT", "colm", n("of")], [n("cr")], act(b("cr"), cw.indirect(b("of")), scale=col(T.colm, row)))
+        new_cast(h, b("Z"), [(M[casts[p]], b("cr", p, CH, 4)) for p in range(4)], [n("Z"), n("cr")] + casts)
+
+    def place(h, t, k):
+        if k == 0:
+            if t == 0: return T.AT[:, :], T.AS[:, :], ["AT"], ["AS"], T.coA, ["coA"]
+            return T.aT[:, :], T.aS[:, :], ["aT0", "aT1"], ["aS0", "aS1"], T.coA, ["coA"]
+        if k == 1:
+            return T.bT[:, :], T.bS[:, :], ["bTx", "bTy", "bT0", "bT1"], ["bSx", "bSy", "bS0", "bS1"], T.coB, ["coBx", "coBy"]
+        return T.hT[:, CW * h:CW * h + CW], T.hS[:, CW * h:CW * h + CW], ["hT%d" % h], ["hS%d" % h], T.coH, ["coH"]
+
+    def fetch(h, t, k):
+        b, n = chunk(h)
+        _, sw, _, sn, _, _ = place(h, t, k)
+        offsets(h, False)
+        S(gat, sn + [n("of")], [n("gS")], act(b("gS"), sw.indirect(b("of"))))
+
+    def hop(h, t, k):
+        b, n = chunk(h)
+        tw, sw, tn, sn, co, cn = place(h, t, k)
+        a0, a1, b0 = col(co, 0), col(co, 1), col(co, 2)
+        pB, pC, pT, pS, dT, dS, gS, of = [b(x) for x in ("pB", "pC", "pT", "pS", "dT", "dS", "gS", "of")]
+        xz = [("RX", n("Z"), b("Z"))]
+        for j, s in enumerate((16, 8, 4, 2, 1)):
+            if j or k == 0: fetch(h, t, k)
+            spread(h, "pB", xz)
+            S(big, [n("pB")] + cn, [n("pB")], act(pB, pB, scale=a1))
+            S(big, [n("pB")] + cn, [n("pB")], act(pB, pB, bias=a0))
+            if j in BOTH_ON_SCALAR:
+                S(gat, tn + [n("of")], [n("dT")], act(dT, tw.indirect(of)))
+                V(big, [n("dT"), n("pT")], [n("dT")], tt(dT, dT, pT, A.subtract))
+            else:
+                V(gtt, tn + [n("of"), n("T1")], [n("dT")], tt(dT, tw.indirect(of), b("T1"), A.subtract))
+            V(big, [n("gS"), n("pS")], [n("dS")], tt(dS, gS, pS, A.subtract))
+            S(big, [n("dS")] + cn, [n("dS")], act(dS, dS, scale=b0))
+            V(big, [n("pB"), n("dT")], [n("pB")], tt(pB, pB, dT, A.mult))
+            count(h, "sg")
+            o = b("pC", 64, 128)
+            PE([n("Z"), n("sg"), "I", "S%d" % s], [n("pC")], [(o, [(M["I"], b("Z")), (M["S%d" % s], b("sg"))])])
+            V(sm, [n("pC"), "CLIP"], [n("Z")], ts(b("Z"), o, 0.0, C["CLIP"], A.max, A.min))
+        offsets(h, True)
+        pair(h, tw, sw, tn, sn)
+        if k == 0: current(h, T.cuT[:, :], 1)
+        elif k == 1: new_cast(h, b("Z"), [(M["I"], T.HC[:, :])], [n("Z"), "I", "HC"])
+        for j in (1, 2, 3):
+            mn, mt = (("M8", T.M8[:, :]), (n("m2"), b("m2")), (n("m3"), b("m3")))[j - 1]
+            tv, sv = b("WT%d" % j), b("WS%d" % j)
+            spread(h, "pB", xz + [("R1", mn, mt)])
+            S(big, [n("pB")] + cn, [n("dT")], act(dT, pB, scale=a1))
+            S(big, [n("dT")] + cn, [n("dT")], act(dT, dT, bias=a0))
+            if j == 1:
+                if k < 2: fetch(h, t, k + 1)
+                S(big, [n("sb")], [n("pC")], act(pC, b("sb"), scale=0.5))
+                S(big, [n("tb")], [n("pB")], act(pB, b("tb"), scale=0.5))
+            else:
+                spread(h, "pC", [("RK", mn, mt)])
+                V(big, [n("pC"), n("tb")], [n("pB")], tt(pB, pC, b("tb"), A.mult))
+                V(big, [n("pC"), n("sb")], [n("pC")], tt(pC, pC, b("sb"), A.mult))
+            V(big, [n("pC"), n("WS0")], [n("WS%d" % j)], tt(sv, pC, b("WS0"), A.add))
+            V(big, [n("WS%d" % j), n("pS")], [n("dS")], tt(dS, sv, pS, A.subtract))
+            S(big, [n("dS")] + cn, [n("dS")], act(dS, dS, scale=b0))
+            V(big, [n("pB"), n("WT0")], [n("WT%d" % j)], tt(tv, pB, b("WT0"), A.add))
+            V(big, [n("WT%d" % j), n("pT")], [n("pB")], tt(pB, tv, pT, A.subtract))
+            V(big, [n("pB"), n("dT")], [n("pB")], tt(pB, pB, dT, A.mult))
+            count(h, "g%d" % j)
+            if j == 1:
+                S(sm, [n("g1")], [n("m2")], act(b("m2"), b("g1"), scale=4.0, bias=8.0))
+            elif j == 2:
+                o = b("pC", 64, 128)
+                PE([n("m2"), n("g2"), "S1", "S2"], [n("pC")], [(o, [(M["S1"], b("m2")), (M["S2"], b("g2"))])])
+                S(sm, [n("pC")], [n("m3")], act(b("m3"), o))
+        o = b("pC", 64, 128)
+        PE([n("g1"), n("g2"), n("g3"), "S1", "SY2", "SY3"], [n("pC")],
+           [(o, [(M["S1"], b("g1")), (M["SY2"], b("g2")), (M["SY3"], b("g3"))])])
+        S(sm, [n("pC")], [n("ys")], act(b("ys"), o, F.Sign, bias=1.0))
+        o, od = b("pC", 128, 144), b("pC", 192, 256)
+        PE([n("ys"), "I", "JJ", n("Z"), n("m3"), n("g3"), "E", "SH"] + every("SA"), [n("pC")],
+           [(o, [(M["SA%d" % a], b("ys", a, 64, 4)) for a in range(4)] + [(M["I"], T.JJ[:, :])]),
+            (od, [(M["E"], b("Z")), (M["SH"], b("m3")), (M["SH"], b("g3"))])])
+        V(sm, [n("pC")], [n("se")], cp(b("se"), o))
+        V(sm, [n("pC"), "QM1"], [n("Z")], ts(b("Z"), od, C["QM1"], None, A.add))
+        wt, ws = b("WT").indirect(b("se")), b("WS").indirect(b("se"))
+        wtn, wsn = [n("WT%d" % j) for j in range(4)] + [n("se")], [n("WS%d" % j) for j in range(4)] + [n("se")]
+        if k < 2:
+            S(gat, wsn, [n("dS")], act(dS, ws))
+            S(gat, wtn, [n("T1")], act(b("T1"), wt))
+            S(big, [n("dS")], [n("pS")], act(pS, dS))
+            S(big, [n("T1")], [n("pT")], act(pT, b("T1")))
+            return
+        for nm, win, wn, tab, bn, bank, u in (("hT", wt, wtn, T.hT, "dT", "pB", 0), ("hS", ws, wsn, T.hS, "dS", "pC", 1)):
+            old = tab[:, CW * h + t:CW * h + CW:4]
+            un, uu = n("U%d" % u), b("U%d" % u)
+            V(gtt, wn + [n(nm)], [n(bn)], tt(b(bn), win, old, A.subtract))
+            S(big, [n(bn)], [n(bank)], act(b(bank), b(bn), scale=0.25))
+            V(big, [n(bank), n(nm)], [un], tt(uu, b(bank), old, A.add))
+            if t == 0: S(big, [un], [n(nm)], act(old, uu))
+            else: dma("Y", [un], [], (T.yt, T.ys)[u][:, CH * h:CH * h + CH], uu, 1 << 17)
+
+    for h in range(NC):
+        b, n = chunk(h)
+        t1, s1_ = T.HT[:, CW * h:CW * h + CW:4], T.HS[:, CW * h:CW * h + CW:4]
+        S(big, ["HT"], [n("T1")], act(b("T1"), t1))
+        S(big, ["HT"], [n("pT")], act(b("pT"), t1))
+        S(big, ["HS"], [n("pS")], act(b("pS"), s1_))
+        new_cast(h, T.L0[:, :], [(M[casts[p]], T.cuT[:, CW * h + 4 * p:CW * h + CW:16]) for p in range(4)], ["L0", "cuT"] + casts)
+    dma("Y", ["ccA"], ["cuT"], T.cuT[1:128:16, :], T.ccA[:, :], 65536)
+    dma("Y", ["dco"], ["coBx"], T.coB[0:112, 0:3], T.dco[16:128, :], 1536)
+    dma("Y", ["dco"], ["coBy"], T.coB[112:128, 0:3], T.dco[0:16, :], 1536)
+    for h in range(NC):
+        for k in range(3): hop(h, 0, k)
+    for u in (0, 1):
+        hs = (2 * u, 2 * u + 1)
+        send(HA, ["U%d%d" % (x, h) for x in (0, 1) for h in hs], ["Lx%d" % u, "Ly%d" % u],
+             T.L1[:, 1024 * u:1024 * u + 1024], T.U[:, 1024 * u:1024 * u + 1024], 1 << 19)
+    send(HB, every("U0") + every("U1"), ["dU"], T.dU[:, :], T.U[:, :], 1 << 20)
+
+    def put(h, tabs, names, more):
+        chunk(h)
+        u = str(h // 2)
+        for x in (0, 1):
+            S(big, ["Lx" + u, "Ly" + u] + more, [names[x] + u], act(tabs[x][:, CW * h:CW * h + CW:4], T.L1[:, (2 * h + x) * CH:(2 * h + x + 1) * CH]))
+    for h in range(NC): put(h, (T.aT, T.aS), ("aT", "aS"), [])
+    dma("Y", ["dU"], ["Lx0", "Lx1"], T.L1[0:112, :], T.dU[16:128, :], 7 << 17)
+    dma("Y", ["dU"], ["Ly0", "Ly1"], T.L1[112:128, :], T.dU[0:16, :], 1 << 17)
+    for h in range(NC):
+        step[h] += 3
+        put(h, (T.bT, T.bS), ("bT", "bS"), ["bTx", "bTy", "bSx", "bSy"])
+        step[h] -= 3
+    for h in range(NC):
+        b, n = chunk(h)
+        o = b("pC", 0, 64)
+        PE([n("Z"), "L0", "HM"], [n("pC")], [(o, [(M["HM"], b("Z")), (M["HM"], T.L0[:, :])])])
+        V(sm, [n("pC")], [n("ia")], cp(b("ia"), o))
+        V(sm, [n("ia")], [n("ib")], ts(b("ib"), b("ia"), 4, None, A.arith_shift_right))
+        V(sm, [n("ib")], [n("dl")], cp(b("dl"), b("ib")))
+        V(sm, [n("ia")], [n("ib")], ts(b("ib"), b("ia"), 15, None, A.bitwise_and))
+        V(sm, [n("ib")], [n("m2")], cp(b("m2"), b("ib")))
+        V(sm, [n("ia")], [n("ia")], ts(b("ia"), b("ia"), 14, None, A.bitwise_and))
+        V(sm, [n("ia")], [n("m3")], cp(b("m3"), b("ia")))
+        o1, o2 = b("pC", 0, 64), b("pC", 64, 128)
+        PE([n("dl"), n("m2"), n("m3"), "E", "SH", "I", "HC"], [n("pC")],
+           [(o1, [(M["E"], b("dl")), (M["I"], T.HC[:, :]), (M["SH"], b("m2"))]), (o2, [(M["E"], b("dl")), (M["SH"], b("m3"))])])
+        V(sm, [n("pC")], [n("Z")], cp(b("Z"), o1))
+        V(sm, [n("pC")], [n("F")], cp(b("F"), o2))
+        offsets(h, True)
+        tw, sw, tn, sn, _, _ = place(h, 1, 2)
+        pair(h, tw, sw, tn, sn)
+        current(h, T.cuT[:, CW * h:CW * h + CW], 0)
+        spread(h, "pB", [("RK", n("m2"), b("m2"))])
+        pB, pT, pS = b("pB"), b("pT"), b("pS")
+        V(big, [n("pB"), n("sb")], [n("pS")], tt(pS, pB, b("sb"), A.mult))
+        V(big, [n("pB"), n("tb")], [n("pT")], tt(pT, pB, b("tb"), A.mult))
+        V(big, [n("pS"), n("WS0")], [n("pS")], tt(pS, pS, b("WS0"), A.add))
+        V(big, [n("pT"), n("WT0")], [n("pT")], tt(pT, pT, b("WT0"), A.add))
+        S(big, [n("pT")], [n("T1")], act(b("T1"), pT))
+        step[h] += 1
+        for k in range(3): hop(h, 1, k)
+        spread(h, "pT", [("RD", n("Z"), b("Z")), ("RD", n("F"), b("F"))])
+        S(big, [n("pT")], [n("gS")], act(b("gS"), pT, scale=0.5))
+        dma("Y", [n("gS")], [], T.yd[:, CH * h:CH * h + CH], T["W%d" % h][0:128:16, 13 * CH:14 * CH], 8192)
+    return ops
+
+
+def arrange(ops, e, order=None):
+    n = len(ops)
+    cost = [cost_ns(o["cost"], e) for o in ops]
+    users = [[] for _ in range(n)]
+    pre = [list(o["deps"]) + list(o["sim"]) for o in ops]
+    for i in range(n):
+        for d in pre[i]: users[d].append(i)
+    span = [cost[i] + (2000 + ops[i]["bytes"] / e["bw"] if ops[i]["kind"] in ("dma", "send") else 0) for i in range(n)]
+    prio = [0.0] * n
+    for i in range(n - 1, -1, -1):
+        prio[i] = span[i] + max([prio[u] + e["lat"] for u in users[i]] + [0.0])
+    for i in range(n):
+        prio[i] = prio[i] * e["pw"] - 1000 * (ops[i]["step"] + e["lead"] * ops[i]["h"]) + (1e6 if ops[i]["cost"] == ("1", 64) else 0)
+    fixed = {q: [i for i in range(n) if ops[i]["eng"] == q] for q in "G"}
+    if order is not None:
+        for q in "VSPY": fixed[q] = order[q]
+    pos = {q: 0 for q in fixed}
+    out = {q: [] for q in "VSPGYX"}
+    free = {q: 0.0 for q in "VSPGYX"}
+    wire = [0.0]
+    left = [len(p) for p in pre]
+    ready = [0.0] * n
+    done = [0.0] * n
+    pool = {q: [i for i in range(n) if ops[i]["eng"] == q and left[i] == 0] for q in "VSPGYX"}
+    todo = n
+    while todo:
+        best = None
+        for q in "VSPGYX":
+            if q in fixed:
+                cand = fixed[q][pos[q]:pos[q] + 1]
+                if cand and left[cand[0]]: cand = []
+            else: cand = pool[q]
+            if not cand: continue
+            t0 = max(free[q], min(ready[i] for i in cand))
+            if q == "Y": i = min((i for i in cand if ready[i] <= t0))
+            else: i = max((i for i in cand if ready[i] <= t0 + e["look"]), key=lambda i: (prio[i], -i))
+            t0 = max(t0, ready[i])
+            if best is None or t0 < best[0]: best = (t0, q, i)
+        t0, q, i = best
+        pool[q].remove(i)
+        if q in pos: pos[q] += 1
+        out[q].append(i)
+        if q != "X": free[q] = t0 + cost[i]
+        fin = t0 + cost[i]
+        if ops[i]["kind"] in ("dma", "send"):
+            wire[0] = max(wire[0], fin + 1300) + ops[i]["bytes"] / e["bw"]
+            fin = wire[0] + 700
+        done[i] = fin
+        todo -= 1
+        for u in users[i]:
+            ready[u] = max(ready[u], fin + e["lat"])
+            left[u] -= 1
+            if left[u] == 0: pool[ops[u]["eng"]].append(u)
+    return out, max(done), done
+
+
+def rank_program(g, core, T, topo):
+    if T.rank_of(core) is None:
+        return
+    ops = plan(g, T, topo, core)
+    order, _, done = arrange(ops, EST)
+    queue = {"V": g.vector, "S": g.scalar, "P": g.tensor, "G": g, "Y": g.sync}
+    token = {}
+    for q in "VSPG":
+        k = 0
+        for i in order[q]:
+            if ops[i]["kind"] == "c":
+                k += 1
+                token[i] = (q, k)
+    for i, o in enumerate(ops):
+        if o["kind"] != "c": token[i] = (o["sem"], o["val"])
+    known = {q: {} for q in queue}
+    clock = {}
+    at = {q: 0 for q in queue}
+    for i in order["X"]: clock[i] = {}
+    going = True
+    while going:
+        going = False
+        for q in queue:
+            while at[q] < len(order[q]) and all(d in clock for d in ops[order[q][at[q]]]["deps"]):
+                i = order[q][at[q]]
+                at[q] += 1
+                going = True
+                kn = known[q]
+                for d in sorted(ops[i]["deps"], key=lambda d: -done[d]):
+                    s, v = token[d]
+                    if kn.get(s, 0) >= v: continue
+                    queue[q].wait_ge(T.sem[s], v)
+                    kn[s] = v
+                    for s2, v2 in clock[d].items():
+                        if kn.get(s2, 0) < v2: kn[s2] = v2
+                clock[i] = dict(kn)
+                ins = ops[i]["fn"]()
+                if ops[i]["kind"] == "c": ins.then_inc(T.sem[q], 1)
+                elif ops[i]["kind"] == "dma": ins.then_inc(T.sem[token[i][0]], 16)
+    top = {}
+    for s, v in token.values(): top[s] = max(top.get(s, 0), v)
+    for s, v in top.items():
+        if known["G"].get(s, 0) < v: g.wait_ge(T.sem[s], v)

@@ -6,6 +6,9 @@ NC = 4
 CH = 256
 W = 4096
 CW = W // NC
+STEPS = (16, 8, 4, 2, 1)
+SHIFT = (16, 24, 28, 30, 31)
+BIG = 1.5 * 2.0 ** 24
 
 SCRATCH = {
     "HT": ("sbuf", [128, W], "bfloat16"), "HS": ("sbuf", [128, W], "bfloat16"),
@@ -21,27 +24,38 @@ SCRATCH = {
     "dco": ("dram", [128, 3], "float32"), "dU": ("dram", [128, 2048], "float32"),
     "pid": ("sbuf", [128, 4], "int32"), "dif": ("sbuf", [128, 128], "float32"), "rel": ("sbuf", [128, 128], "float32"),
     "BD": ("sbuf", [128, 128], "float32"), "tmp": ("sbuf", [128, 128], "float32"),
-    "cf": ("sbuf", [128, 24], "float32"), "colm": ("sbuf", [128, 16], "float32"), "cold": ("sbuf", [128, 16], "float32"),
+    "cf": ("sbuf", [128, 32], "float32"), "colm": ("sbuf", [128, 16], "float32"), "cold": ("sbuf", [128, 24], "float32"),
     "cq": ("sbuf", [128, 4], "float32"),
     "i0": ("sbuf", [128, 64], "float32"), "i1": ("sbuf", [128, 64], "float32"), "i2": ("sbuf", [128, 16], "float32"),
     "MH": ("sbuf", [128, 17 * 128], "float16"),
-    "MB": ("sbuf", [128, 28 * 128], "bfloat16"),
-    "L0": ("sbuf", [128, 64], "float16"), "HC": ("sbuf", [128, 64], "float16"), "JJ": ("sbuf", [128, 16], "float16"),
-    "M8": ("sbuf", [128, 64], "bfloat16"),
+    "MB": ("sbuf", [128, 47 * 128], "bfloat16"),
+    "MF": ("sbuf", [128, 3 * 128], "float32"),
+    "L0": ("sbuf", [128, 64], "float16"), "HC": ("sbuf", [128, 64], "float16"),
+    "KS": ("sbuf", [128, 2 * 64], "bfloat16"),
+    "ONE": ("sbuf", [128, 2 * CH], "bfloat16"),
 }
 for _h in range(NC):
-    SCRATCH["W%d" % _h] = ("sbuf", [128, 14 * CH], "float32")
-    SCRATCH["B%d" % _h] = ("sbuf", [128, 2 * CH + 7 * 64], "bfloat16")
+    SCRATCH["W%d" % _h] = ("sbuf", [128, 10 * CH], "float32")
+    SCRATCH["B%d" % _h] = ("sbuf", [128, 5 * CH + 3 * 64], "bfloat16")
     SCRATCH["H%d" % _h] = ("sbuf", [128, 3 * 64], "float16")
     SCRATCH["I%d" % _h] = ("sbuf", [128, 2 * 64], "int32")
-    SCRATCH["O%d" % _h] = ("sbuf", [128, 3 * 16], "uint16")
+    SCRATCH["O%d" % _h] = ("sbuf", [128, 2 * 16], "uint16")
     SCRATCH["P%d" % _h] = ("psum", [128, 2 * CH], "float32")
     SCRATCH["Q%d" % _h] = ("psum", [128, 2 * CH], "float32")
 
 SEMAPHORES = ["V", "S", "P", "G"] + ["d%d" % _k for _k in range(40)] + ["l%d" % _k for _k in range(14)] + ["r%d" % _k for _k in range(14)]
 
-EST = {"cyc": 0.83, "gat": 1.56, "pe": 0.42, "lat": 160.0, "bw": 300.0, "lead": 1.5, "pw": 1.0, "look": 0.0}
-BOTH_ON_SCALAR = ()
+EST = {"cyc": 0.83, "gat": 1.56, "pe": 0.55, "lat": 250.0, "bw": 200.0, "lead": 2.0, "iss": 1500.0, "dl": 2000.0}
+SHARE = [
+    [{"both": (), "ps": 5, "fps": 0, "wv": (), "T": "AAA", "S": "AAA", "first": "AAA", "end": "AA"}],
+    [{"both": (), "ps": 5, "wv": (), "T": "VVV", "S": "VAA", "end": "VV"}],
+]
+
+
+def share_of(t, h): return SHARE[t][h % len(SHARE[t])]
+
+
+def ps_of(t, k, h): return share_of(t, h)["fps" if t == 0 and k == 0 else "ps"]
 
 
 def cost_ns(c, e):
@@ -50,7 +64,8 @@ def cost_ns(c, e):
     if k == "h": return max(64, n / 2) * e["cyc"]
     if k == "2": return max(64, 2 * n) * e["cyc"]
     if k == "g": return 65 + n * e["gat"] * e["cyc"]
-    if k == "t": return 50 + n * e.get("tt", e["gat"]) * e["cyc"]
+    if k == "t": return 50 + n * e["gat"] * e["cyc"]
+    if k == "i": return n * e["iss"]
     if k == "pe": return n * e["pe"]
     return n
 
@@ -60,20 +75,30 @@ def plan(g, T, topo, core):
     F = ActivationFunctionType
     rank = T.rank_of(core)
     ops = []
-    last, readers, banks = {}, {}, {}
+    last, readers, banks, opened = {}, {}, {}, {}
     cnt = {"d": 0, "r": 0, "h": 0}
     step = [0] * NC
     bank_of = {"pT": "P", "pB": "P", "pS": "Q", "pC": "Q"}
 
-    def op(eng, cost, reads, writes, fn, kind="c", after=(), nbytes=0, sem=None, val=0):
+    def op(eng, cost, reads, writes, fn, kind="c", after=(), nbytes=0, sem=None, val=0, group=None):
         i = len(ops)
         deps = set(after)
+        touched = set(bank_of[x[:2]] + x[2:] for x in reads + writes if x[:2] in bank_of)
+        for bk in touched:
+            if bk[0] != "P": continue
+            if group in ("open", "stop"):
+                assert opened.get(bk, False) == (group == "stop")
+                opened[bk] = group == "open"
+                writes = writes + ["group" + bk]
+            else:
+                assert opened.get(bk, False) == (group == "in")
+                reads = reads + ["group" + bk]
         for r in reads:
             if r in last: deps.add(last[r])
         for w in writes:
             if w in last: deps.add(last[w])
             deps.update(readers.get(w, ()))
-        for bk in set(bank_of[x[:2]] + x[2:] for x in reads + writes if x[:2] in bank_of):
+        for bk in touched:
             who, now, before = banks.get(bk, (eng, [], []))
             if who != eng: now, before = [], now
             deps.update(before)
@@ -83,12 +108,13 @@ def plan(g, T, topo, core):
             last[w] = i
             readers[w] = []
         deps.discard(i)
-        ops.append({"eng": eng, "cost": cost, "deps": deps, "fn": fn, "kind": kind, "bytes": nbytes, "sem": sem, "val": val, "sim": (),
+        soft = set(d for d in deps if eng == "P" and ops[d]["eng"] == "P" and group in ("in", "stop"))
+        ops.append({"eng": eng, "cost": cost, "deps": deps, "fn": fn, "kind": kind, "bytes": nbytes, "sem": sem, "val": val, "sim": (), "soft": soft,
                     "h": cnt["h"], "step": step[cnt["h"]]})
         return i
 
-    def V(cost, reads, writes, fn): return op("V", cost, reads, writes, fn)
-    def S(cost, reads, writes, fn): return op("S", cost, reads, writes, fn)
+    def V(cost, reads, writes, fn, group=None): return op("V", cost, reads, writes, fn, group=group)
+    def S(cost, reads, writes, fn, group=None): return op("S", cost, reads, writes, fn, group=group)
 
     def ts(out, in0, s1, s2, o0, o1=None):
         if o1 is None: return lambda: g.vector.tensor_scalar(out, in0, s1, None, o0)
@@ -96,14 +122,14 @@ def plan(g, T, topo, core):
     def tt(out, a, b, o): return lambda: g.vector.tensor_tensor(out, a, b, o)
     def cp(out, a): return lambda: g.vector.tensor_copy(out, a)
     def act(out, a, f=None, **kw): return lambda: g.scalar.activation(out, a, F.Identity if f is None else f, **kw)
+    def keep(out, a): return lambda: g.affine_select(out, a, [[0, CH]], A.is_ge, 0.0, 0, 0)
 
-    def PE(reads, writes, groups, onto=False, cycles=None, one=False):
+    def PE(reads, writes, groups, cycles=None):
         def fn():
             ins = None
-            for x, (out, terms) in enumerate(groups):
+            for out, terms in groups:
                 for k, (l, r) in enumerate(terms):
-                    ins = g.tensor.matmul(out, l, r, k == 0 and not onto and not (one and x),
-                                          k == len(terms) - 1 and not one)
+                    ins = g.tensor.matmul(out, l, r, k == 0, k == len(terms) - 1)
             return ins
         return op("P", ("pe", cycles or 64 * sum(len(t) for _, t in groups)), reads, writes, fn)
 
@@ -111,7 +137,7 @@ def plan(g, T, topo, core):
         sem = "d%d" % cnt["d"]
         cnt["d"] += 1
         e = g if q == "G" else g.sync
-        return op(q, ("n", 1000.0 if q == "G" else 100.0), reads, writes, lambda: e.dma_start(out, in_), "dma", after, nbytes, sem, 16)
+        return op(q, ("i", 1.0) if q == "G" else ("n", 100.0), reads, writes, lambda: e.dma_start(out, in_), "dma", after, nbytes, sem, 16)
 
     def send(away, reads, writes, out, in_, nbytes, after=()):
         k = cnt["r"]
@@ -120,7 +146,7 @@ def plan(g, T, topo, core):
         src = T.cores[(rank + away) % N]
         rid, pid, _ = topo.addr(dst)
         m = topo.mask(core, dst)
-        i = op("G", ("n", 1000.0), reads, [], lambda: g.remote_dma(out, in_, T.sem["r%d" % k], T.sem["l%d" % k], pid, rid, m),
+        i = op("G", ("i", 1.0), reads, [], lambda: g.remote_dma(out, in_, T.sem["r%d" % k], T.sem["l%d" % k], pid, rid, m),
                "send", after, nbytes, "l%d" % k, len(topo.engines(core, dst)))
         j = op("X", ("n", 0.0), [], writes, None, "land", (), 0, "r%d" % k, len(topo.engines(src, core)))
         ops[j]["deps"] = set()
@@ -131,8 +157,8 @@ def plan(g, T, topo, core):
     def every(x): return [x + str(h) for h in range(NC)]
 
     dma("Y", [], ["coH"], T.coH[:, 0:3], T.co[:, :], 1536)
-    dma("Y", [], ["cui"], T.cui[:, :], T.cu[:, :], 131072)
     dma("Y", [], ["HT"], T.HT[:, :], T.te[:, :], 1 << 20)
+    dma("Y", [], ["cui"], T.cui[:, :], T.cu[:, :], 131072)
     dma("Y", [], ["HS"], T.HS[:, :], T.sa[:, :], 1 << 20)
 
     def numbers(name, out, pat, cm):
@@ -159,11 +185,12 @@ def plan(g, T, topo, core):
         dma("G", [dn], [nm + "y"], tab[112:128, :], src[0:16, :], 1 << 18)
     dma("G", [], every("hT"), T.hT[:, :], T.te[:, :], 2 << 20)
     dma("G", [], every("hS"), T.hS[:, :], T.sa[:, :], 2 << 20)
-    dma("G", ["AT"], ["aT0", "aT1"], T.aT[:, :], T.AT[:, :], 2 << 20)
-    dma("G", ["AS"], ["aS0", "aS1"], T.aS[:, :], T.AS[:, :], 2 << 20)
+    dma("G", ["AT"], every("aT"), T.aT[:, :], T.AT[:, :], 2 << 20)
+    dma("G", ["AS"], every("aS"), T.aS[:, :], T.AS[:, :], 2 << 20)
 
     c1, c128 = ("1", 1), ("1", 128)
-    names = ["PIDF", "Q", "Q3", "QC", "C0", "C1", "C2", "C3", "CLIP", "QM1", "HMC", "SELW", "Q4", "LOW", "KEEP", "EVEN", "x0", "x1"]
+    names = ["PIDF", "Q", "Q3", "QC", "C0", "C1", "C2", "C3", "HMC", "Q4", "LOW", "KEEP", "EVEN", "x0", "x1", "MB4", "MB2"]
+    names += ["LO%d" % j for j in range(5)] + ["HI%d" % j for j in range(5)]
     C = {nm: col(T.cf, k) for k, nm in enumerate(names)}
 
     def column(nm, src, s1, s2, o0, o1=None):
@@ -176,12 +203,14 @@ def plan(g, T, topo, core):
     V(c1, ["iq3"], ["Q3"], cp(C["Q3"], col(T.pid, 2)))
     column("QC", "Q", "Q3", 0.25, A.subtract, A.mult)
     for k in range(4): column("C%d" % k, "QC", float(k), None, A.is_equal)
-    column("CLIP", "C0", -3586.0, 4096.0, A.mult, A.add)
-    column("QM1", "C3", -1.0, None, A.mult)
+    for j, s in enumerate(SHIFT):
+        column("LO%d" % j, "C0", 4096.0 + s, -4096.0, A.mult, A.add)
+        column("HI%d" % j, "C0", s - 3586.0, 4096.0, A.mult, A.add)
     column("x0", "C3", 0.5, None, A.mult)
     column("HMC", "C2", 8.0, "x0", A.mult, A.add)
-    column("x1", "C1", 2.0 * CH / 2, None, A.mult)
-    column("SELW", "C0", CH / 2, "x1", A.mult, A.add)
+    column("x1", "C1", -8.0, None, A.mult)
+    column("MB4", "C0", 4.0, "x1", A.mult, A.add)
+    column("MB2", "C0", -2.0, "x1", A.mult, A.add)
     column("Q4", "Q3", 4.0, None, A.mult)
     column("LOW", "QC", 1.5, None, A.is_lt)
     column("KEEP", "QC", 1.0, None, A.not_equal)
@@ -196,23 +225,37 @@ def plan(g, T, topo, core):
     V(c1, ["colm", "cd0"], ["cd"], tt(T.cold[:, 4:8], T.cold[:, 0:4], T.colm[:, 12:16], A.add))
     V(c1, ["colm"], ["cx0"], ts(T.cold[:, 8:12], T.colm[:, 0:4], 16.0, None, A.mult))
     V(c1, ["cd", "cx0"], ["cx"], tt(T.cold[:, 12:16], T.cold[:, 8:12], T.cold[:, 4:8], A.add))
+    V(c1, ["colm"], ["cm"], tt(T.cold[:, 16:20], T.colm[:, 0:4], T.colm[:, 4:8], A.add))
+    V(c1, ["colm"], ["ck"], ts(T.cold[:, 20:24], T.colm[:, 0:4], 0.0625, None, A.mult))
     V(c1, ["i2", "Q3"], ["cq"], ts(T.cq[:, :], T.i2[:, 0:4], 0.25, C["Q3"], A.mult, A.add))
     M = {}
     for k, nm in enumerate(["I", "KP", "E", "HM", "E0"] + every("RX") + every("RD") + every("MA")):
         M[nm] = T.MH[:, 128 * k:128 * k + 128]
-    for k, nm in enumerate(["CN%d" % p for p in range(8)] + every("R1") + every("RK") + every("SA") + ["S16", "S8", "S4", "S2", "S1", "SH", "SY2", "SY3"]):
+    counts = {s: ["N%d_%d" % (s, p) for p in range(4)] for s in STEPS}
+    casts = every("NC")
+    single = ["S16", "S8", "S4", "S2", "S1", "SH", "I2", "J2", "U16", "U8", "U4", "U2", "U1", "U0", "BK"]
+    for k, nm in enumerate(sum(counts.values(), []) + casts + every("R1") + every("RK") + single):
         M[nm] = T.MB[:, 128 * k:128 * k + 128]
-    for p in range(8):
-        V(c128, ["rel"], ["CN%d" % p], ts(M["CN%d" % p], rel, float(p), None, A.is_equal))
+    M["I4"], M["J4"], M["H4"] = T.MF[:, 0:128], T.MF[:, 128:256], T.MF[:, 256:384]
     for p in range(4):
         x = str(p)
+        V(c128, ["rel"], [casts[p]], ts(M[casts[p]], rel, float(4 + p), None, A.is_equal))
+        V(c128, ["rel"], [counts[8][p]], ts(M[counts[8][p]], rel, float(p), None, A.is_equal))
+        for s in (16, 4, 2, 1):
+            S(c128, [counts[8][p]], [counts[s][p]], act(M[counts[s][p]], M[counts[8][p]], scale=s / 8.0))
         V(c128, ["BD", "cx"], ["RX" + x], ts(M["RX" + x], BD, col(T.cold, 12 + p), None, A.mult))
         V(c128, ["BD", "cd"], ["RD" + x], ts(M["RD" + x], BD, col(T.cold, 4 + p), None, A.mult))
-        S(c128, ["BD", "colm"], ["R1" + x], act(M["R1" + x], BD, scale=col(T.colm, p)))
-        S(c128, ["R1" + x], ["RK" + x], act(M["RK" + x], M["R1" + x], scale=0.0625))
+        S(c128, ["BD", "cm"], ["R1" + x], act(M["R1" + x], BD, scale=col(T.cold, 16 + p)))
+        S(c128, ["BD", "ck"], ["RK" + x], act(M["RK" + x], BD, scale=col(T.cold, 20 + p)))
         V(c128, ["rel", "cq", "LOW"], ["MA" + x], ts(M["MA" + x], rel, col(T.cq, p), C["LOW"], A.is_equal, A.mult))
-        V(c128, ["rel", "cq", "SELW"], ["SA" + x], ts(M["SA" + x], rel, col(T.cq, p), C["SELW"], A.is_equal, A.mult))
     V(c128, ["dif"], ["I"], ts(M["I"], dif, 0.0, None, A.is_equal))
+    V(c128, ["dif"], ["I4"], ts(M["I4"], dif, 0.0, None, A.is_equal))
+    if any(c in "BD" for r in SHARE for x in r for c in x["T"] + x["S"]) or any(x["ps"] < 5 for r in SHARE for x in r):
+        S(c128, ["I4"], ["J4"], act(M["J4"], M["I4"], scale=-1.0))
+    if any(c in "CD" for r in SHARE for x in r for c in x["T"] + x["S"] + x.get("first", "")):
+        S(c128, ["I4"], ["H4"], act(M["H4"], M["I4"], scale=0.5))
+    S(c128, ["I4"], ["I2"], act(M["I2"], M["I4"]))
+    S(c128, ["I4"], ["J2"], act(M["J2"], M["I4"], scale=-1.0))
     V(c128, ["dif", "KEEP"], ["KP"], ts(M["KP"], dif, 0.0, C["KEEP"], A.is_equal, A.mult))
     V(c128, ["dif", "LOW"], ["E"], ts(M["E"], dif, 0.0, C["LOW"], A.is_equal, A.mult))
     V(c128, ["dif", "C0"], ["E0"], ts(M["E0"], dif, 8.0, C["C0"], A.is_equal, A.mult))
@@ -221,14 +264,27 @@ def plan(g, T, topo, core):
     V(c128, ["dif", "C0"], ["S1"], ts(M["S1"], dif, 0.0, C["C0"], A.is_equal, A.mult))
     for s in (16, 8, 4, 2):
         S(c128, ["S1"], ["S%d" % s], act(M["S%d" % s], M["S1"], scale=float(s)))
+    V(c128, ["dif", "C1"], ["U0"], ts(M["U0"], dif, 4.0, C["C1"], A.is_equal, A.mult))
+    V(c128, ["dif", "C1"], ["BK"], ts(M["BK"], dif, -4.0, C["C1"], A.is_equal, A.mult))
+    V(("2", 128), ["BK", "U0"], ["BK"], tt(M["BK"], M["BK"], M["U0"], A.add))
+    S(c128, ["BK"], ["BK"], act(M["BK"], M["BK"], scale=-float(SHIFT[4])))
+    V(("2", 128), ["S1", "U0"], ["U1"], tt(M["U1"], M["S1"], M["U0"], A.subtract))
+    for s in (16, 8, 4, 2):
+        S(c128, ["U1"], ["U%d" % s], act(M["U%d" % s], M["U1"], scale=float(s)))
+    V(c128, ["dif", "C1"], ["U0"], ts(M["U0"], dif, 8.0, C["C1"], A.is_equal, A.mult))
+    S(c128, ["U0"], ["U0"], act(M["U0"], M["U0"], scale=8.0))
+    V(("2", 128), ["U1", "U0"], ["U1"], tt(M["U1"], M["U1"], M["U0"], A.add))
     V(c128, ["dif", "C0"], ["SH"], ts(M["SH"], dif, 12.0, C["C0"], A.is_equal, A.mult))
-    V(c128, ["dif", "C0"], ["SY3"], ts(M["SY3"], dif, 4.0, C["C0"], A.is_equal, A.mult))
-    V(("2", 128), ["SY3", "S1"], ["SY2"], tt(M["SY2"], M["SY3"], M["S1"], A.subtract))
-    V(("2", 128), ["SY3", "S2"], ["SY3"], tt(M["SY3"], M["SY3"], M["S2"], A.add))
     V(c1, ["i0", "Q4", "EVEN"], ["L0"], ts(T.L0[:, :], T.i0[:, :], C["Q4"], C["EVEN"], A.add, A.mult))
     V(c1, ["i1", "C1"], ["HC"], ts(T.HC[:, :], T.i1[:, :], C["C1"], None, A.mult))
-    V(c1, ["i2", "Q"], ["JJ"], ts(T.JJ[:, :], T.i2[:, :], C["Q"], 1.5 * CH, A.add, A.add))
-    V(c1, [], ["M8"], lambda: g.vector.memset(T.M8[:, :], 8.0))
+    K = {}
+
+    def fill(nm, ap, value):
+        K[nm] = ap
+        V(c128, [], [nm], lambda: g.vector.memset(ap, value))
+    for k, (nm, value) in enumerate((("DOWN", -BIG), ("UP", BIG))): fill(nm, T.KS[:, 64 * k:64 * k + 64], value)
+    V(c1, ["UP", "C0", "C1"], ["UP"], ts(K["UP"], K["UP"], C["C0"], C["C1"], A.mult, A.add))
+    fill("ONE", T.ONE[0:1, :], 1.0)
 
     big, gat, gtt, sm = ("1", CH), ("g", CH), ("t", CH), ("1", 64)
 
@@ -236,15 +292,14 @@ def plan(g, T, topo, core):
         cnt["h"] = h
         x = str(h)
         at = {}
-        for k, nm in enumerate(["WT0", "WT1", "WT2", "WT3", "WS0", "WS1", "WS2", "WS3", "tb", "sb", "T1", "dT", "dS", "gS"]):
-            at[nm] = (T["W" + x], k * CH, CH)
-        at["WT"], at["WS"] = (T["W" + x], 0, 4 * CH), (T["W" + x], 4 * CH, 4 * CH)
-        at["vo"], at["cr"] = (T["B" + x], 0, CH), (T["B" + x], CH, CH)
-        for k, nm in enumerate(["sg", "g1", "g2", "g3", "m2", "m3", "ys"]): at[nm] = (T["B" + x], 2 * CH + 64 * k, 64)
+        for k, nm in enumerate(["ta", "sa", "tb", "sb", "T1", "S1", "gT", "gS", "dS", "w"]): at[nm] = (T["W" + x], k * CH, CH)
+        for k, nm in enumerate(["vo", "cr", "t2", "s2", "g2"]): at[nm] = (T["B" + x], k * CH, CH)
+        for k, nm in enumerate(["m2", "m3", "mq"]): at[nm] = (T["B" + x], 5 * CH + 64 * k, 64)
         for k, nm in enumerate(["Z", "F", "dl"]): at[nm] = (T["H" + x], 64 * k, 64)
         for k, nm in enumerate(["ia", "ib"]): at[nm] = (T["I" + x], 64 * k, 64)
-        for k, nm in enumerate(["of", "og", "se"]): at[nm] = (T["O" + x], 16 * k, 16)
+        for k, nm in enumerate(["of", "og"]): at[nm] = (T["O" + x], 16 * k, 16)
         at["pT"], at["pB"], at["pS"], at["pC"] = (T["P" + x], 0, CH), (T["P" + x], CH, CH), (T["Q" + x], 0, CH), (T["Q" + x], CH, CH)
+        at["PP"] = (T["P" + x], 0, 2 * CH)
         at["U0"], at["U1"] = (T.U, 2 * CH * h, CH), (T.U, 2 * CH * h + CH, CH)
 
         def b(nm, first=0, end=None, by=1):
@@ -253,172 +308,235 @@ def plan(g, T, topo, core):
             return t[:, o + first:o + (w if end is None else end):by]
         return b, (lambda nm: nm + x)
 
-    def spread(h, bank, parts, one=False):
+    def spread(h, bank, parts):
         b, n = chunk(h)
         reads = []
         for f, nm, _ in parts: reads += [nm] + every(f)
-        PE(reads, [n(bank)], [(b(bank, p, CH, 4), [(M[f + str(p)], t) for f, _, t in parts]) for p in range(4)], one=one)
+        PE(reads, [n(bank)], [(b(bank, p, CH, 4), [(M[f + str(p)], t) for f, _, t in parts]) for p in range(4)])
 
-    def offsets(h, both):
-        b, n = chunk(h)
-        o = b("pC", 128, 144)
-        PE([n("Z")] + every("MA"), [n("pC")], [(o, [(M["MA%d" % a], b("Z", a, 64, 4)) for a in range(4)])])
-        V(sm, [n("pC")], [n("of")], cp(b("of"), o))
-        if both: V(sm, [n("pC")], [n("og")], ts(b("og"), o, 1.0, None, A.add))
+    def cycles(terms): return sum(CH * (4 if x[0][1] == "4" else 1) for x in terms)
 
-    def new_cast(h, src, terms, reads):
+    def start(h, regions):
         b, n = chunk(h)
-        o = b("pC", 64, 128)
-        PE(reads + ["KP"], [n("pC")], [(o, [(M["KP"], src)] + terms)])
-        V(sm, [n("pC")], [n("Z")], cp(b("Z"), o))
+        out = b(regions[0]) if len(regions) == 1 else b("PP")
+        wide = CH * len(regions)
+        op("P", ("pe", wide), ["ONE"], [n(x) for x in regions],
+           lambda: g.tensor.matmul(out, T.ONE[0:1, 0:128], T.ONE[0:1, 0:wide], True, False), group="open")
 
-    def count(h, sg):
+    def onto(h, region, terms, reads, stop):
         b, n = chunk(h)
-        o = b("pC", 0, 64)
-        V(big, [n("pB"), n("dS")], [n("vo")], tt(b("vo"), b("pB"), b("dS"), A.is_gt))
-        PE([n("vo")] + every("CN"), [n("pC")], [(o, [(M["CN%d" % p], b("vo", p, CH, 4)) for p in range(4)])])
+
+        def fn():
+            ins = None
+            for k, (lhs, rhs) in enumerate(terms): ins = g.tensor.matmul(b(region), M[lhs], rhs, False, stop and k == len(terms) - 1)
+            return ins
+        op("P", ("pe", cycles(terms)), reads + [x[0] for x in terms], [n(region)], fn, group="stop" if stop else "in")
+
+    def sums(h, region, terms, reads):
+        b, n = chunk(h)
+        PE(reads + [x[0] for x in terms], [n(region)], [(b(region), [(M[l], r) for l, r in terms])], cycles(terms))
+
+    def offsets(h, both, region, shift=0):
+        b, n = chunk(h)
+        o = b(region, 128, 144)
+        PE([n("Z")] + every("MA"), [n(region)], [(o, [(M["MA%d" % a], b("Z", a, 64, 4)) for a in range(4)])])
+        V(sm, [n(region)], [n("of")], ts(b("of"), o, -float(shift), None, A.add))
+        if both: V(sm, [n(region)], [n("og")], ts(b("og"), o, 1.0 - shift, None, A.add))
+
+    def new_cast(h, src, terms, reads, region):
+        b, n = chunk(h)
+        o = b(region, 64, 128)
+        PE(reads + ["KP"], [n(region)], [(o, [(M["KP"], src)] + terms)])
+        V(sm, [n(region)], [n("Z")], cp(b("Z"), o))
+
+    def vote(h, left, right, s, region, up, more, reads):
+        b, n = chunk(h)
+        o = b(region, 0, 64)
+        x = "S%d" % s
+        V(big, [n(left), n(right)], [n("vo")], tt(b("vo"), b(left), b(right), A.is_gt))
+        PE([n("vo"), x, up, "UP", "DOWN"] + counts[s] + reads, [n(region)],
+           [(o, [(M[up], K["UP"])] + [(M[counts[s][p]], b("vo", p, CH, 4)) for p in range(4)] + [(M[x], K["DOWN"])] + more)])
         step[h] += 1
-        S(sm, [n("pC")], [n(sg)], act(b(sg), o, F.Sign, bias=-8.5))
+        return o
 
-    def pair(h, tw, sw, tn, sn):
+    def pair(h, t, tw, sw, tn, sn):
         b, n = chunk(h)
-        S(gat, sn + [n("of")], [n("WS0")], act(b("WS0"), sw.indirect(b("of"))))
-        S(gat, tn + [n("of")], [n("WT0")], act(b("WT0"), tw.indirect(b("of"))))
-        V(gtt, sn + [n("og"), n("WS0")], [n("sb")], tt(b("sb"), sw.indirect(b("og")), b("WS0"), A.subtract))
-        V(gtt, tn + [n("og"), n("WT0")], [n("tb")], tt(b("tb"), tw.indirect(b("og")), b("WT0"), A.subtract))
-
-    casts = ["CN4", "CN5", "CN6", "CN7"]
+        ta, sa = (("t2", "s2"), ("ta", "sa"))[t]
+        S(gat, sn + [n("of")], [n(sa)], act(b(sa), sw.indirect(b("of"))))
+        S(gat, tn + [n("of")], [n(ta)], act(b(ta), tw.indirect(b("of"))))
+        V(gtt, sn + [n("og"), n(sa)], [n("sb")], tt(b("sb"), sw.indirect(b("og")), b(sa), A.subtract))
+        V(gtt, tn + [n("og"), n(ta)], [n("tb")], tt(b("tb"), tw.indirect(b("og")), b(ta), A.subtract))
 
     def current(h, cw, row):
         b, n = chunk(h)
         S(gat, ["cuT", "colm", n("of")], [n("cr")], act(b("cr"), cw.indirect(b("of")), scale=col(T.colm, row)))
-        new_cast(h, b("Z"), [(M[casts[p]], b("cr", p, CH, 4)) for p in range(4)], [n("Z"), n("cr")] + casts)
+
+    def carried(h, region):
+        b, n = chunk(h)
+        new_cast(h, b("Z"), [(M[casts[p]], b("cr", p, CH, 4)) for p in range(4)], [n("Z"), n("cr")] + casts, region)
 
     def place(h, t, k):
         if k == 0:
             if t == 0: return T.AT[:, :], T.AS[:, :], ["AT"], ["AS"], T.coA, ["coA"]
-            return T.aT[:, :], T.aS[:, :], ["aT0", "aT1"], ["aS0", "aS1"], T.coA, ["coA"]
+            return T.aT[:, :], T.aS[:, :], every("aT"), every("aS"), T.coA, ["coA"]
         if k == 1:
-            return T.bT[:, :], T.bS[:, :], ["bTx", "bTy", "bT0", "bT1"], ["bSx", "bSy", "bS0", "bS1"], T.coB, ["coBx", "coBy"]
+            return T.bT[:, :], T.bS[:, :], ["bTx", "bTy"] + every("bT"), ["bSx", "bSy"] + every("bS"), T.coB, ["coBx", "coBy"]
         return T.hT[:, CW * h:CW * h + CW], T.hS[:, CW * h:CW * h + CW], ["hT%d" % h], ["hS%d" % h], T.coH, ["coH"]
 
-    def fetch(h, t, k):
+    def fetch(h, t, k, j, region):
         b, n = chunk(h)
-        _, sw, _, sn, _, _ = place(h, t, k)
-        offsets(h, False)
-        S(gat, sn + [n("of")], [n("gS")], act(b("gS"), sw.indirect(b("of"))))
+        tw, sw, tn, sn, _, _ = place(h, t, k)
+        offsets(h, False, region, SHIFT[j - 1] if j or k else 0)
+        gs = "g2" if t == 0 and j >= ps_of(t, k, h) else "gS"
+        S(gat, sn + [n("of")], [n(gs)], act(b(gs), sw.indirect(b("of"))))
+        if j == 0 or j in share_of(t, h)["both"]: S(gat, tn + [n("of")], [n("gT")], act(b("gT"), tw.indirect(b("of"))))
+
+    def between(h, t, modes, kk, less, where):
+        b, n = chunk(h)
+        ta, sa = (("t2", "s2"), ("ta", "sa"))[t]
+        wide = "24"[t]
+        tr, sr = where
+        sides = [(sr, "sb", sa, modes[1], less[1]), (tr, "tb", ta, modes[0], less[0])]
+        for r, d, a, mode, (x, xn, xw) in sides:
+            if mode in "CD":
+                terms = [("H4", b(d)), ("I" + wide, b(a))] + ([("J" + xw, x)] if mode == "D" else [])
+                sums(h, r, terms, [n(d), n(a)] + (xn if mode == "D" else []))
+        sides = [x for x in sides if x[3] not in "CD"]
+        inside = [x[0] for x in sides if x[3] != "V"]
+        if inside: start(h, inside)
+        for r, d, _, mode, _ in sides:
+            gr = "in" if inside else None
+            if kk is None: V(big, [n("pC"), n(d)], [n(r)], tt(b(r), b("pC"), b(d), A.mult), gr)
+            else: S(big, [n(d)], [n(r)], act(b(r), b(d), scale=kk), gr)
+        for r, _, a, mode, (x, xn, xw) in sides:
+            if mode == "V": continue
+            onto(h, r, [("I" + wide, b(a))] + ([("J" + xw, x)] if mode == "B" else []), [n(a)] + (xn if mode == "B" else []), r == inside[-1])
+        for r, _, a, mode, _ in sides:
+            if mode == "V": V(big, [n(r), n(a)], [n(r)], tt(b(r), b(r), b(a), A.add))
+
+    def settle(h, t):
+        b, n = chunk(h)
+        modes = share_of(t, h)["end"]
+        none = (None, None, None)
+        sr = "pS" if modes[1] == "V" else "pB"
+        between(h, t, modes, None, (none, none), ("pT", sr))
+        if share_of(t, h)["ps"] == 0: S(big, [n(sr)], [n("S1")], act(b("S1"), b(sr)))
+        elif sr != "pS": S(big, [n(sr)], [n("pS")], act(b("pS"), b(sr)))
 
     def hop(h, t, k):
         b, n = chunk(h)
+        share = share_of(t, h)
         tw, sw, tn, sn, co, cn = place(h, t, k)
         a0, a1, b0 = col(co, 0), col(co, 1), col(co, 2)
-        pB, pC, pT, pS, dT, dS, gS, of = [b(x) for x in ("pB", "pC", "pT", "pS", "dT", "dS", "gS", "of")]
+        pB, pT, pS, dS, gT, gS, w, of = [b(x) for x in ("pB", "pT", "pS", "dS", "gT", "gS", "w", "of")]
+        t1, s1 = (b("T1"), [n("T1")], "4"), (b("S1"), [n("S1")], "4")
+        first = t == 0 and k == 0
+        if first: t1, s1 = (T.HT[:, CW * h:CW * h + CW:4], ["HT"], "2"), (T.HS[:, CW * h:CW * h + CW:4], ["HS"], "2")
         xz = [("RX", n("Z"), b("Z"))]
-        for j, s in enumerate((16, 8, 4, 2, 1)):
-            if j or k == 0: fetch(h, t, k)
-            spread(h, "pB", xz)
-            S(big, [n("pB")] + cn, [n("pB")], act(pB, pB, scale=a1))
-            S(big, [n("pB")] + cn, [n("pB")], act(pB, pB, bias=a0))
-            if j in BOTH_ON_SCALAR:
-                S(gat, tn + [n("of")], [n("dT")], act(dT, tw.indirect(of)))
-                V(big, [n("dT"), n("pT")], [n("dT")], tt(dT, dT, pT, A.subtract))
+
+        def weight(test, x, out):
+            if test in share["wv"]: V(big, [n(x)] + cn, [n(out)], ts(b(out), b(x), a1, a0, A.mult, A.add))
             else:
-                V(gtt, tn + [n("of"), n("T1")], [n("dT")], tt(dT, tw.indirect(of), b("T1"), A.subtract))
-            V(big, [n("gS"), n("pS")], [n("dS")], tt(dS, gS, pS, A.subtract))
-            S(big, [n("dS")] + cn, [n("dS")], act(dS, dS, scale=b0))
-            V(big, [n("pB"), n("dT")], [n("pB")], tt(pB, pB, dT, A.mult))
-            count(h, "sg")
-            o = b("pC", 64, 128)
-            PE([n("Z"), n("sg"), "I", "S%d" % s], [n("pC")], [(o, [(M["I"], b("Z")), (M["S%d" % s], b("sg"))])])
-            V(sm, [n("pC"), "CLIP"], [n("Z")], ts(b("Z"), o, 0.0, C["CLIP"], A.max, A.min))
-        offsets(h, True)
-        pair(h, tw, sw, tn, sn)
+                S(big, [n(x)] + cn, [n(out)], act(b(out), b(x), scale=a1))
+                S(big, [n(out)] + cn, [n(out)], act(b(out), b(out), bias=a0))
+
+        for j, s in enumerate(STEPS):
+            early = j == 0 and k > 0
+            if early:
+                spread(h, "pC", xz)
+                weight(j, "pC", "w")
+            else:
+                fetch(h, t, k, j, "pC")
+                spread(h, "pB", xz)
+                weight(j, "pB", "pB")
+            if j >= ps_of(t, k, h):
+                gs = ("g2", "gS")[t]
+                sums(h, "pS", [("I" + "24"[t], b(gs)), ("J" + s1[2], s1[0])], [n(gs)] + s1[1])
+                S(big, [n("pS")] + cn, [n("dS")], act(dS, pS, scale=b0))
+            else:
+                V(big, [n("gS"), n("pS")], [n("dS")], tt(dS, gS, pS, A.subtract))
+                S(big, [n("dS")] + cn, [n("dS")], act(dS, dS, scale=b0))
+            if j == 0 and not first and share["ps"]: S(big, [n("pS")], [n("S1")], act(b("S1"), pS))
+            if early:
+                V(big, [n("gT"), n("pT")], [n("pB")], tt(pB, gT, pT, A.subtract))
+                V(big, [n("pB"), n("w")], [n("pB")], tt(pB, pB, w, A.mult))
+            else:
+                if j == 0 or j in share["both"]: V(big, [n("gT"), n("pT")], [n("gT")], tt(gT, gT, pT, A.subtract))
+                else: V(gtt, tn + [n("of")] + t1[1], [n("gT")], tt(gT, tw.indirect(of), t1[0], A.subtract))
+                V(big, [n("pB"), n("gT")], [n("pB")], tt(pB, pB, gT, A.mult))
+            o = vote(h, "pB", "dS", s, "pC", "U%d" % s, [(M["I"], b("Z"))], [n("Z"), "I"])
+            if j == 0 and not first: S(big, [n("pT")], [n("T1")], act(b("T1"), pT))
+            V(sm, [n("pC"), "LO%d" % j, "HI%d" % j], [n("Z")], ts(b("Z"), o, C["LO%d" % j], C["HI%d" % j], A.max, A.min))
+        offsets(h, True, "pC", SHIFT[4])
         if k == 0: current(h, T.cuT[:, :], 1)
-        elif k == 1: new_cast(h, b("Z"), [(M["I"], T.HC[:, :])], [n("Z"), "I", "HC"])
-        for j in (1, 2, 3):
-            mn, mt = (("M8", T.M8[:, :]), (n("m2"), b("m2")), (n("m3"), b("m3")))[j - 1]
-            tv, sv = b("WT%d" % j), b("WS%d" % j)
-            spread(h, "pB", xz + [("R1", mn, mt)])
-            S(big, [n("pB")] + cn, [n("dT")], act(dT, pB, scale=a1))
-            S(big, [n("dT")] + cn, [n("dT")], act(dT, dT, bias=a0))
-            if j == 1:
-                if k < 2: fetch(h, t, k + 1)
-                S(big, [n("sb")], [n("pC")], act(pC, b("sb"), scale=0.5))
-                S(big, [n("tb")], [n("pB")], act(pB, b("tb"), scale=0.5))
+        pair(h, t, tw, sw, tn, sn)
+        for j, s in enumerate((4, 2, 1)):
+            mt = (None, (n("m2"), b("m2")), (n("m3"), b("m3")))[j]
+            modes = share["first"][j] * 2 if first else share["T"][j] + share["S"][j]
+            tr, sr = ("pS" if modes[0] == "V" and modes[1] != "V" else "pT"), "pB"
+            if j: spread(h, "pC", [("RK",) + mt])
+            spread(h, "pS", xz + ([("R1",) + mt] if j else []))
+            if tr == "pS" or j == 0: weight(5 + j, "pS", "w")
+            if j == 0 and k < 2:
+                if k == 0: carried(h, "pC")
+                else: new_cast(h, b("Z"), [(M["I"], T.HC[:, :])], [n("Z"), "I", "HC"], "pC")
+                fetch(h, t, k + 1, 0, "pC")
+            between(h, t, modes, None if j else 0.5, (t1, s1), (tr, sr))
+            if tr != "pS" and j: weight(5 + j, "pS", "w")
+            if modes[1] in "BD": S(big, [n(sr)] + cn, [n("dS")], act(dS, b(sr), scale=b0))
             else:
-                spread(h, "pC", [("RK", mn, mt)])
-                V(big, [n("pC"), n("tb")], [n("pB")], tt(pB, pC, b("tb"), A.mult))
-                V(big, [n("pC"), n("sb")], [n("pC")], tt(pC, pC, b("sb"), A.mult))
-            V(big, [n("pC"), n("WS0")], [n("WS%d" % j)], tt(sv, pC, b("WS0"), A.add))
-            V(big, [n("WS%d" % j), n("pS")], [n("dS")], tt(dS, sv, pS, A.subtract))
-            S(big, [n("dS")] + cn, [n("dS")], act(dS, dS, scale=b0))
-            V(big, [n("pB"), n("WT0")], [n("WT%d" % j)], tt(tv, pB, b("WT0"), A.add))
-            V(big, [n("WT%d" % j), n("pT")], [n("pB")], tt(pB, tv, pT, A.subtract))
-            V(big, [n("pB"), n("dT")], [n("pB")], tt(pB, pB, dT, A.mult))
-            count(h, "g%d" % j)
-            if j == 1:
-                S(sm, [n("g1")], [n("m2")], act(b("m2"), b("g1"), scale=4.0, bias=8.0))
-            elif j == 2:
-                o = b("pC", 64, 128)
-                PE([n("m2"), n("g2"), "S1", "S2"], [n("pC")], [(o, [(M["S1"], b("m2")), (M["S2"], b("g2"))])])
-                S(sm, [n("pC")], [n("m3")], act(b("m3"), o))
-        o = b("pC", 64, 128)
-        PE([n("g1"), n("g2"), n("g3"), "S1", "SY2", "SY3"], [n("pC")],
-           [(o, [(M["S1"], b("g1")), (M["SY2"], b("g2")), (M["SY3"], b("g3"))])])
-        S(sm, [n("pC")], [n("ys")], act(b("ys"), o, F.Sign, bias=1.0))
-        o, od = b("pC", 128, 144), b("pC", 192, 256)
-        PE([n("ys"), "I", "JJ", n("Z"), n("m3"), n("g3"), "E", "SH"] + every("SA"), [n("pC")],
-           [(o, [(M["SA%d" % a], b("ys", a, 64, 4)) for a in range(4)] + [(M["I"], T.JJ[:, :])]),
-            (od, [(M["E"], b("Z")), (M["SH"], b("m3")), (M["SH"], b("g3"))])])
-        V(sm, [n("pC")], [n("se")], cp(b("se"), o))
-        V(sm, [n("pC"), "QM1"], [n("Z")], ts(b("Z"), od, C["QM1"], None, A.add))
-        wt, ws = b("WT").indirect(b("se")), b("WS").indirect(b("se"))
-        wtn, wsn = [n("WT%d" % j) for j in range(4)] + [n("se")], [n("WS%d" % j) for j in range(4)] + [n("se")]
+                V(big, [n(sr)] + s1[1], [n("dS")], tt(dS, b(sr), s1[0], A.subtract))
+                S(big, [n("dS")] + cn, [n("dS")], act(dS, dS, scale=b0))
+            if modes[0] not in "BD": V(big, [n(tr)] + t1[1], [n(tr)], tt(b(tr), b(tr), t1[0], A.subtract))
+            V(big, [n(tr), n("w")], [n(tr)], tt(b(tr), b(tr), w, A.mult))
+            o = vote(h, tr, "dS", s, "pC", "S%d" % s, [(M["S1"], mt[1])] if j else [], [mt[0], "S1"] if j else [])
+            nxt, mb = ("m2", "m3", "mq")[j], ("MB4", "MB2", "MB2")[j]
+            S(sm, [n("pC"), mb], [n(nxt)], act(b(nxt), o, bias=C[mb]))
+        zr = "pB" if k < 2 and share["end"][1] == "V" else "pS"
+        o = b(zr, 64, 128)
+        spread(h, "pC", [("RK", n("mq"), b("mq"))])
+        PE([n("Z"), n("mq"), "E", "SH", "BK", "UP"], [n(zr)], [(o, [(M["E"], b("Z")), (M["SH"], b("mq")), (M["BK"], K["UP"])])])
+        V(sm, [n(zr)], [n("Z")], cp(b("Z"), o))
         if k < 2:
-            S(gat, wsn, [n("dS")], act(dS, ws))
-            S(gat, wtn, [n("T1")], act(b("T1"), wt))
-            S(big, [n("dS")], [n("pS")], act(pS, dS))
-            S(big, [n("T1")], [n("pT")], act(pT, b("T1")))
+            settle(h, t)
             return
-        for nm, win, wn, tab, bn, bank, u in (("hT", wt, wtn, T.hT, "dT", "pB", 0), ("hS", ws, wsn, T.hS, "dS", "pC", 1)):
-            old = tab[:, CW * h + t:CW * h + CW:4]
+        olds = [(tab[:, CW * h + t:CW * h + CW:4], [nm], "2") for tab, nm in ((T.HT, "HT"), (T.HS, "HS"))]
+        regions = ("pT", "pB")
+        between(h, t, "BB", None, olds, regions)
+        for u in (1, 0): S(big, [n(regions[u])], [n(regions[u])], act(b(regions[u]), b(regions[u]), scale=0.25))
+        for u in (1, 0):
+            r, (old, on, _) = regions[u], olds[u]
             un, uu = n("U%d" % u), b("U%d" % u)
-            V(gtt, wn + [n(nm)], [n(bn)], tt(b(bn), win, old, A.subtract))
-            S(big, [n(bn)], [n(bank)], act(b(bank), b(bn), scale=0.25))
-            V(big, [n(bank), n(nm)], [un], tt(uu, b(bank), old, A.add))
-            if t == 0: S(big, [un], [n(nm)], act(old, uu))
+            V(big, [n(r)] + on, [un], tt(uu, b(r), old, A.add))
+            if t == 0: S(big, [un], [n(("hT", "hS")[u])], act((T.hT, T.hS)[u][:, CW * h:CW * h + CW:4], uu))
             else: dma("Y", [un], [], (T.yt, T.ys)[u][:, CH * h:CH * h + CH], uu, 1 << 17)
 
     for h in range(NC):
         b, n = chunk(h)
-        t1, s1_ = T.HT[:, CW * h:CW * h + CW:4], T.HS[:, CW * h:CW * h + CW:4]
-        S(big, ["HT"], [n("T1")], act(b("T1"), t1))
-        S(big, ["HT"], [n("pT")], act(b("pT"), t1))
-        S(big, ["HS"], [n("pS")], act(b("pS"), s1_))
-        new_cast(h, T.L0[:, :], [(M[casts[p]], T.cuT[:, CW * h + 4 * p:CW * h + CW:16]) for p in range(4)], ["L0", "cuT"] + casts)
+        S(big, ["HT"], [n("pT")], act(b("pT"), T.HT[:, CW * h:CW * h + CW:4]))
+        if ps_of(0, 0, h): S(big, ["HS"], [n("pS")], act(b("pS"), T.HS[:, CW * h:CW * h + CW:4]))
+        new_cast(h, T.L0[:, :], [(M[casts[p]], T.cuT[:, CW * h + 4 * p:CW * h + CW:16]) for p in range(4)], ["L0", "cuT"] + casts, "pC")
     dma("Y", ["ccA"], ["cuT"], T.cuT[1:128:16, :], T.ccA[:, :], 65536)
     dma("Y", ["dco"], ["coBx"], T.coB[0:112, 0:3], T.dco[16:128, :], 1536)
     dma("Y", ["dco"], ["coBy"], T.coB[112:128, 0:3], T.dco[0:16, :], 1536)
     for h in range(NC):
         for k in range(3): hop(h, 0, k)
-    for u in (0, 1):
-        hs = (2 * u, 2 * u + 1)
-        send(HA, ["U%d%d" % (x, h) for x in (0, 1) for h in hs], ["Lx%d" % u, "Ly%d" % u],
-             T.L1[:, 1024 * u:1024 * u + 1024], T.U[:, 1024 * u:1024 * u + 1024], 1 << 19)
+    for h in range(NC):
+        send(HA, ["U0%d" % h, "U1%d" % h], ["Lx%d" % h, "Ly%d" % h],
+             T.L1[:, 2 * CH * h:2 * CH * (h + 1)], T.U[:, 2 * CH * h:2 * CH * (h + 1)], 1 << 18)
     send(HB, every("U0") + every("U1"), ["dU"], T.dU[:, :], T.U[:, :], 1 << 20)
 
-    def put(h, tabs, names, more):
+    def put(h, tabs, names, more, pool):
         chunk(h)
-        u = str(h // 2)
+        u = str(h)
         for x in (0, 1):
-            S(big, ["Lx" + u, "Ly" + u] + more, [names[x] + u], act(tabs[x][:, CW * h:CW * h + CW:4], T.L1[:, (2 * h + x) * CH:(2 * h + x + 1) * CH]))
-    for h in range(NC): put(h, (T.aT, T.aS), ("aT", "aS"), [])
-    dma("Y", ["dU"], ["Lx0", "Lx1"], T.L1[0:112, :], T.dU[16:128, :], 7 << 17)
-    dma("Y", ["dU"], ["Ly0", "Ly1"], T.L1[112:128, :], T.dU[0:16, :], 1 << 17)
-    for h in range(NC):
-        step[h] += 3
-        put(h, (T.bT, T.bS), ("bT", "bS"), ["bTx", "bTy", "bSx", "bSy"])
-        step[h] -= 3
+            out, in_ = tabs[x][:, CW * h:CW * h + CW:4], T.L1[:, (2 * h + x) * CH:(2 * h + x + 1) * CH]
+            if pool: op("G", ("n", 170 + 2 * CH * 0.83), ["Lx" + u, "Ly" + u] + more, [names[x] + u], keep(out, in_))
+            else: S(big, ["Lx" + u, "Ly" + u] + more, [names[x] + u], act(out, in_))
+    for h in range(NC): put(h, (T.aT, T.aS), ("aT", "aS"), [], False)
+    dma("Y", ["dU"], every("Lx"), T.L1[0:112, :], T.dU[16:128, :], 7 << 17)
+    dma("Y", ["dU"], every("Ly"), T.L1[112:128, :], T.dU[0:16, :], 1 << 17)
+    for h in range(NC): put(h, (T.bT, T.bS), ("bT", "bS"), ["bTx", "bTy", "bSx", "bSy"], True)
     for h in range(NC):
         b, n = chunk(h)
         o = b("pC", 0, 64)
@@ -435,38 +553,40 @@ def plan(g, T, topo, core):
            [(o1, [(M["E"], b("dl")), (M["I"], T.HC[:, :]), (M["SH"], b("m2"))]), (o2, [(M["E"], b("dl")), (M["SH"], b("m3"))])])
         V(sm, [n("pC")], [n("Z")], cp(b("Z"), o1))
         V(sm, [n("pC")], [n("F")], cp(b("F"), o2))
-        offsets(h, True)
+        offsets(h, True, "pC")
         tw, sw, tn, sn, _, _ = place(h, 1, 2)
-        pair(h, tw, sw, tn, sn)
+        pair(h, 1, tw, sw, tn, sn)
         current(h, T.cuT[:, CW * h:CW * h + CW], 0)
-        spread(h, "pB", [("RK", n("m2"), b("m2"))])
-        pB, pT, pS = b("pB"), b("pT"), b("pS")
-        V(big, [n("pB"), n("sb")], [n("pS")], tt(pS, pB, b("sb"), A.mult))
-        V(big, [n("pB"), n("tb")], [n("pT")], tt(pT, pB, b("tb"), A.mult))
-        V(big, [n("pS"), n("WS0")], [n("pS")], tt(pS, pS, b("WS0"), A.add))
-        V(big, [n("pT"), n("WT0")], [n("pT")], tt(pT, pT, b("WT0"), A.add))
-        S(big, [n("pT")], [n("T1")], act(b("T1"), pT))
+        carried(h, "pB" if share_of(1, h)["end"][1] == "V" else "pS")
+        spread(h, "pC", [("RK", n("m2"), b("m2"))])
+        settle(h, 1)
         step[h] += 1
         for k in range(3): hop(h, 1, k)
-        spread(h, "pT", [("RD", n("Z"), b("Z")), ("RD", n("F"), b("F"))])
-        S(big, [n("pT")], [n("gS")], act(b("gS"), pT, scale=0.5))
-        dma("Y", [n("gS")], [], T.yd[:, CH * h:CH * h + CH], T["W%d" % h][0:128:16, 13 * CH:14 * CH], 8192)
+        spread(h, "pC", [("RD", n("Z"), b("Z")), ("RD", n("F"), b("F"))])
+        S(big, [n("pC")], [n("gS")], act(b("gS"), b("pC"), scale=0.5))
+        dma("Y", [n("gS")], [], T.yd[:, CH * h:CH * h + CH], T["W%d" % h][0:128:16, 7 * CH:8 * CH], 8192)
     return ops
 
 
-def arrange(ops, e, order=None):
-    n = len(ops)
+def spans(ops, e):
     cost = [cost_ns(o["cost"], e) for o in ops]
+    span = [c + (700 + e["dl"] + o["bytes"] / e["bw"] if o["kind"] in ("dma", "send") else 0) for c, o in zip(cost, ops)]
+    return cost, span, [list(o["deps"]) + list(o["sim"]) for o in ops]
+
+
+def arrange(ops, e, order=None, given=None):
+    n = len(ops)
+    cost, span, pre = spans(ops, e)
     users = [[] for _ in range(n)]
-    pre = [list(o["deps"]) + list(o["sim"]) for o in ops]
     for i in range(n):
         for d in pre[i]: users[d].append(i)
-    span = [cost[i] + (2000 + ops[i]["bytes"] / e["bw"] if ops[i]["kind"] in ("dma", "send") else 0) for i in range(n)]
-    prio = [0.0] * n
-    for i in range(n - 1, -1, -1):
-        prio[i] = span[i] + max([prio[u] + e["lat"] for u in users[i]] + [0.0])
-    for i in range(n):
-        prio[i] = prio[i] * e["pw"] - 1000 * (ops[i]["step"] + e["lead"] * ops[i]["h"]) + (1e6 if ops[i]["cost"] == ("1", 64) else 0)
+    prio = given
+    if prio is None:
+        prio = [0.0] * n
+        for i in range(n - 1, -1, -1):
+            prio[i] = span[i] + max([prio[u] + e["lat"] for u in users[i]] + [0.0])
+        for i in range(n):
+            prio[i] += (1e6 if ops[i]["cost"] == ("1", 64) else 0) - 1000 * (ops[i]["step"] + e["lead"] * ops[i]["h"])
     fixed = {q: [i for i in range(n) if ops[i]["eng"] == q] for q in "G"}
     if order is not None:
         for q in "VSPY": fixed[q] = order[q]
@@ -478,8 +598,7 @@ def arrange(ops, e, order=None):
     ready = [0.0] * n
     done = [0.0] * n
     pool = {q: [i for i in range(n) if ops[i]["eng"] == q and left[i] == 0] for q in "VSPGYX"}
-    todo = n
-    while todo:
+    for _ in range(n):
         best = None
         for q in "VSPGYX":
             if q in fixed:
@@ -489,8 +608,7 @@ def arrange(ops, e, order=None):
             if not cand: continue
             t0 = max(free[q], min(ready[i] for i in cand))
             if q == "Y": i = min((i for i in cand if ready[i] <= t0))
-            else: i = max((i for i in cand if ready[i] <= t0 + e["look"]), key=lambda i: (prio[i], -i))
-            t0 = max(t0, ready[i])
+            else: i = max((i for i in cand if ready[i] <= t0), key=lambda i: (prio[i], -i))
             if best is None or t0 < best[0]: best = (t0, q, i)
         t0, q, i = best
         pool[q].remove(i)
@@ -499,15 +617,43 @@ def arrange(ops, e, order=None):
         if q != "X": free[q] = t0 + cost[i]
         fin = t0 + cost[i]
         if ops[i]["kind"] in ("dma", "send"):
-            wire[0] = max(wire[0], fin + 1300) + ops[i]["bytes"] / e["bw"]
+            wire[0] = max(wire[0], fin + e["dl"]) + ops[i]["bytes"] / e["bw"]
             fin = wire[0] + 700
         done[i] = fin
-        todo -= 1
         for u in users[i]:
-            ready[u] = max(ready[u], fin + e["lat"])
+            ready[u] = max(ready[u], fin + (0.0 if i in ops[u]["soft"] else e["lat"]))
             left[u] -= 1
             if left[u] == 0: pool[ops[u]["eng"]].append(u)
     return out, max(done), done
+
+
+def backward(ops, e, done):
+    n = len(ops)
+    cost, span, pre = spans(ops, e)
+    lane = [o["eng"] if o["eng"] in "VSP" else "O" for o in ops]
+    left = [0] * n
+    for i in range(n):
+        for d in pre[i]: left[d] += 1
+    free = {q: 0.0 for q in "VSPO"}
+    ready = [0.0] * n
+    fin = [0.0] * n
+    pool = {q: [i for i in range(n) if left[i] == 0 and lane[i] == q] for q in "VSPO"}
+    for _ in range(n):
+        best = None
+        for q in "VSPO":
+            if not pool[q]: continue
+            t0 = max(free[q], min(ready[i] for i in pool[q]))
+            i = max((i for i in pool[q] if ready[i] <= t0), key=lambda i: (done[i], i))
+            if best is None or t0 < best[0]: best = (t0, q, i)
+        t0, q, i = best
+        pool[q].remove(i)
+        if q != "O": free[q] = t0 + cost[i]
+        fin[i] = t0 + span[i]
+        for d in pre[i]:
+            ready[d] = max(ready[d], fin[i] + (0.0 if d in ops[i]["soft"] else e["lat"]))
+            left[d] -= 1
+            if left[d] == 0: pool[lane[d]].append(d)
+    return fin
 
 
 def rank_program(g, core, T, topo):
@@ -515,6 +661,7 @@ def rank_program(g, core, T, topo):
         return
     ops = plan(g, T, topo, core)
     order, _, done = arrange(ops, EST)
+    for _ in range(2): order, _, done = arrange(ops, EST, given=backward(ops, EST, done))
     queue = {"V": g.vector, "S": g.scalar, "P": g.tensor, "G": g, "Y": g.sync}
     token = {}
     for q in "VSPG":
@@ -540,7 +687,7 @@ def rank_program(g, core, T, topo):
                 kn = known[q]
                 for d in sorted(ops[i]["deps"], key=lambda d: -done[d]):
                     s, v = token[d]
-                    if kn.get(s, 0) >= v: continue
+                    if kn.get(s, 0) >= v or d in ops[i]["soft"]: continue
                     queue[q].wait_ge(T.sem[s], v)
                     kn[s] = v
                     for s2, v2 in clock[d].items():

from concourse.mybir import AluOpType, ActivationFunctionType

N = 8
HA, HB = 3, 5
NC = 4
CH = 256
W = 4096
CW = W // NC
STEPS = (16, 8, 4, 2, 1)
SHIFT = (16, 24, 28, 30, 31)
BIG = 1.5 * 2.0 ** 24

SCRATCH = {
    "HT": ("sbuf", [128, W], "bfloat16"), "HS": ("sbuf", [128, W], "bfloat16"),
    "AT": ("sbuf", [128, W], "bfloat16"), "AS": ("sbuf", [128, W], "bfloat16"),
    "hT": ("sbuf", [128, W], "float32"), "hS": ("sbuf", [128, W], "float32"),
    "aT": ("sbuf", [128, W], "float32"), "aS": ("sbuf", [128, W], "float32"),
    "bT": ("sbuf", [128, W], "float32"), "bS": ("sbuf", [128, W], "float32"),
    "cuT": ("sbuf", [128, W], "bfloat16"),
    "cui": ("sbuf", [128, 256], "int32"), "cc": ("sbuf", [128, 256], "bfloat16"), "ccA": ("sbuf", [128, 256], "bfloat16"),
    "coH": ("sbuf", [128, 4], "float32"), "coA": ("sbuf", [128, 4], "float32"), "coB": ("sbuf", [128, 4], "float32"),
    "U": ("sbuf", [128, 2048], "float32"), "L1": ("sbuf", [128, 2048], "float32"),
    "dBT": ("dram", [128, W], "bfloat16"), "dBS": ("dram", [128, W], "bfloat16"),
    "dco": ("dram", [128, 3], "float32"), "dU": ("dram", [128, 2048], "float32"),
    "pid": ("sbuf", [128, 4], "int32"), "dif": ("sbuf", [128, 128], "float32"), "rel": ("sbuf", [128, 128], "float32"),
    "BD": ("sbuf", [128, 128], "float32"), "tmp": ("sbuf", [128, 128], "float32"),
    "cf": ("sbuf", [128, 32], "float32"), "colm": ("sbuf", [128, 16], "float32"), "cold": ("sbuf", [128, 24], "float32"),
    "cq": ("sbuf", [128, 4], "float32"),
    "i0": ("sbuf", [128, 64], "float32"), "i1": ("sbuf", [128, 64], "float32"), "i2": ("sbuf", [128, 16], "float32"),
    "MH": ("sbuf", [128, 17 * 128], "float16"),
    "MB": ("sbuf", [128, 47 * 128], "bfloat16"),
    "MF": ("sbuf", [128, 3 * 128], "float32"),
    "L0": ("sbuf", [128, 64], "float16"), "HC": ("sbuf", [128, 64], "float16"),
    "KS": ("sbuf", [128, 2 * 64], "bfloat16"),
    "ONE": ("sbuf", [128, 2 * CH], "bfloat16"),
}
for _h in range(NC):
    SCRATCH["W%d" % _h] = ("sbuf", [128, 10 * CH], "float32")
    SCRATCH["B%d" % _h] = ("sbuf", [128, 5 * CH + 3 * 64], "bfloat16")
    SCRATCH["H%d" % _h] = ("sbuf", [128, 3 * 64], "float16")
    SCRATCH["I%d" % _h] = ("sbuf", [128, 2 * 64], "int32")
    SCRATCH["O%d" % _h] = ("sbuf", [128, 2 * 16], "uint16")
    SCRATCH["P%d" % _h] = ("psum", [128, 2 * CH], "float32")
    SCRATCH["Q%d" % _h] = ("psum", [128, 2 * CH], "float32")

SEMAPHORES = ["V", "S", "P", "G"] + ["d%d" % _k for _k in range(40)] + ["l%d" % _k for _k in range(14)] + ["r%d" % _k for _k in range(14)]

EST = {"cyc": 0.83, "gat": 1.56, "pe": 0.55, "lat": 250.0, "bw": 200.0, "lead": 2.0, "iss": 1500.0, "dl": 2000.0}
SHARE = [
    [{"both": (), "ps": 5, "fps": 0, "wv": (), "T": "AAA", "S": "AAA", "first": "AAA", "end": "AA"}],
    [{"both": (), "ps": 5, "wv": (), "T": "VVV", "S": "VAA", "end": "VV"}],
]


def share_of(t, h): return SHARE[t][h % len(SHARE[t])]


def ps_of(t, k, h): return share_of(t, h)["fps" if t == 0 and k == 0 else "ps"]


def cost_ns(c, e):
    k, n = c
    if k == "1": return max(64, n) * e["cyc"]
    if k == "h": return max(64, n / 2) * e["cyc"]
    if k == "2": return max(64, 2 * n) * e["cyc"]
    if k == "g": return 65 + n * e["gat"] * e["cyc"]
    if k == "t": return 50 + n * e["gat"] * e["cyc"]
    if k == "i": return n * e["iss"]
    if k == "pe": return n * e["pe"]
    return n


def plan(g, T, topo, core):
    A = AluOpType
    F = ActivationFunctionType
    rank = T.rank_of(core)
    ops = []
    last, readers, banks, opened = {}, {}, {}, {}
    cnt = {"d": 0, "r": 0, "h": 0}
    step = [0] * NC
    bank_of = {"pT": "P", "pB": "P", "pS": "Q", "pC": "Q"}

    def op(eng, cost, reads, writes, fn, kind="c", after=(), nbytes=0, sem=None, val=0, group=None):
        i = len(ops)
        deps = set(after)
        touched = set(bank_of[x[:2]] + x[2:] for x in reads + writes if x[:2] in bank_of)
        for bk in touched:
            if bk[0] != "P": continue
            if group in ("open", "stop"):
                assert opened.get(bk, False) == (group == "stop")
                opened[bk] = group == "open"
                writes = writes + ["group" + bk]
            else:
                assert opened.get(bk, False) == (group == "in")
                reads = reads + ["group" + bk]
        for r in reads:
            if r in last: deps.add(last[r])
        for w in writes:
            if w in last: deps.add(last[w])
            deps.update(readers.get(w, ()))
        for bk in touched:
            who, now, before = banks.get(bk, (eng, [], []))
            if who != eng: now, before = [], now
            deps.update(before)
            banks[bk] = (eng, now + [i], before)
        for r in reads: readers.setdefault(r, []).append(i)
        for w in writes:
            last[w] = i
            readers[w] = []
        deps.discard(i)
        soft = set(d for d in deps if eng == "P" and ops[d]["eng"] == "P" and group in ("in", "stop"))
        ops.append({"eng": eng, "cost": cost, "deps": deps, "fn": fn, "kind": kind, "bytes": nbytes, "sem": sem, "val": val, "sim": (), "soft": soft,
                    "h": cnt["h"], "step": step[cnt["h"]]})
        return i

    def V(cost, reads, writes, fn, group=None): return op("V", cost, reads, writes, fn, group=group)
    def S(cost, reads, writes, fn, group=None): return op("S", cost, reads, writes, fn, group=group)

    def ts(out, in0, s1, s2, o0, o1=None):
        if o1 is None: return lambda: g.vector.tensor_scalar(out, in0, s1, None, o0)
        return lambda: g.vector.tensor_scalar(out, in0, s1, s2, o0, o1)
    def tt(out, a, b, o): return lambda: g.vector.tensor_tensor(out, a, b, o)
    def cp(out, a): return lambda: g.vector.tensor_copy(out, a)
    def act(out, a, f=None, **kw): return lambda: g.scalar.activation(out, a, F.Identity if f is None else f, **kw)
    def keep(out, a): return lambda: g.affine_select(out, a, [[0, CH]], A.is_ge, 0.0, 0, 0)

    def PE(reads, writes, groups, cycles=None):
        def fn():
            ins = None
            for out, terms in groups:
                for k, (l, r) in enumerate(terms):
                    ins = g.tensor.matmul(out, l, r, k == 0, k == len(terms) - 1)
            return ins
        return op("P", ("pe", cycles or 64 * sum(len(t) for _, t in groups)), reads, writes, fn)

    def dma(q, reads, writes, out, in_, nbytes, after=()):
        sem = "d%d" % cnt["d"]
        cnt["d"] += 1
        e = g if q == "G" else g.sync
        return op(q, ("i", 1.0) if q == "G" else ("n", 100.0), reads, writes, lambda: e.dma_start(out, in_), "dma", after, nbytes, sem, 16)

    def send(away, reads, writes, out, in_, nbytes, after=()):
        k = cnt["r"]
        cnt["r"] += 1
        dst = T.cores[(rank - away) % N]
        src = T.cores[(rank + away) % N]
        rid, pid, _ = topo.addr(dst)
        m = topo.mask(core, dst)
        i = op("G", ("i", 1.0), reads, [], lambda: g.remote_dma(out, in_, T.sem["r%d" % k], T.sem["l%d" % k], pid, rid, m),
               "send", after, nbytes, "l%d" % k, len(topo.engines(core, dst)))
        j = op("X", ("n", 0.0), [], writes, None, "land", (), 0, "r%d" % k, len(topo.engines(src, core)))
        ops[j]["deps"] = set()
        ops[j]["sim"] = (i,)
        return i

    def col(t, k): return t[:, k:k + 1]
    def every(x): return [x + str(h) for h in range(NC)]

    dma("Y", [], ["coH"], T.coH[:, 0:3], T.co[:, :], 1536)
    dma("Y", [], ["HT"], T.HT[:, :], T.te[:, :], 1 << 20)
    dma("Y", [], ["cui"], T.cui[:, :], T.cu[:, :], 131072)
    dma("Y", [], ["HS"], T.HS[:, :], T.sa[:, :], 1 << 20)

    def numbers(name, out, pat, cm):
        op("G", ("n", 300.0), [], [name], lambda: g.iota(out, pat, 0, cm, allow_small_or_imprecise_dtypes=True))
    op("G", ("n", 140.0), [], ["pid"], lambda: g.iota(T.pid[:, 0:1], [[0, 1]], 0, 1))
    numbers("dif", T.dif[:, :], [[1, 128]], -1)
    numbers("i0", T.i0[:, :], [[0, 2], [16, 32]], 0)
    numbers("i1", T.i1[:, :], [[512, 2], [0, 32]], 0)
    numbers("i2", T.i2[:, :], [[16, 16]], 0)

    V(("h", W), [], ["cuT"], lambda: g.vector.memset(T.cuT[:, :], 0.0))
    V(("1", 256), ["cui"], ["cc"], ts(T.cc[:, :], T.cui[:, :], 512.0, None, A.mult))
    dma("Y", ["cc"], ["cuT"], T.cuT[0:128:16, :], T.cc[:, :], 65536)

    send(HA, ["coH"], ["coA"], T.coA[:, 0:3], T.coH[:, 0:3], 1536)
    s1 = send(HA, ["HT"], ["AT"], T.AT[:, :], T.HT[:, :], 1 << 20)
    s2 = send(HA, ["HS"], ["AS"], T.AS[:, :], T.HS[:, :], 1 << 20)
    send(HA, ["cc"], ["ccA"], T.ccA[:, :], T.cc[:, :], 65536)
    send(HB, ["coH"], ["dco"], T.dco[:, :], T.coH[:, 0:3], 1536, (s1, s2))
    send(HB, ["HT"], ["dBT"], T.dBT[:, :], T.HT[:, :], 1 << 20)
    send(HB, ["HS"], ["dBS"], T.dBS[:, :], T.HS[:, :], 1 << 20)
    for nm, dn, tab, src in (("bT", "dBT", T.bT, T.dBT), ("bS", "dBS", T.bS, T.dBS)):
        dma("G", [dn], [nm + "x"], tab[0:112, :], src[16:128, :], 7 << 18)
        dma("G", [dn], [nm + "y"], tab[112:128, :], src[0:16, :], 1 << 18)
    dma("G", [], every("hT"), T.hT[:, :], T.te[:, :], 2 << 20)
    dma("G", [], every("hS"), T.hS[:, :], T.sa[:, :], 2 << 20)
    dma("G", ["AT"], every("aT"), T.aT[:, :], T.AT[:, :], 2 << 20)
    dma("G", ["AS"], every("aS"), T.aS[:, :], T.AS[:, :], 2 << 20)

    c1, c128 = ("1", 1), ("1", 128)
    names = ["PIDF", "Q", "Q3", "QC", "C0", "C1", "C2", "C3", "HMC", "Q4", "LOW", "KEEP", "EVEN", "x0", "x1", "MB4", "MB2"]
    names += ["LO%d" % j for j in range(5)] + ["HI%d" % j for j in range(5)]
    C = {nm: col(T.cf, k) for k, nm in enumerate(names)}

    def column(nm, src, s1, s2, o0, o1=None):
        rd = [src] + [s for s in (s1, s2) if isinstance(s, str)]
        V(c1, rd, [nm], ts(C[nm], C[src], C.get(s1, s1), C.get(s2, s2), o0, o1))
    V(c1, ["pid"], ["PIDF"], cp(C["PIDF"], col(T.pid, 0)))
    V(c1, ["pid"], ["iq"], ts(col(T.pid, 1), col(T.pid, 0), 15, None, A.bitwise_and))
    V(c1, ["pid"], ["iq3"], ts(col(T.pid, 2), col(T.pid, 0), 3, None, A.bitwise_and))
    V(c1, ["iq"], ["Q"], cp(C["Q"], col(T.pid, 1)))
    V(c1, ["iq3"], ["Q3"], cp(C["Q3"], col(T.pid, 2)))
    column("QC", "Q", "Q3", 0.25, A.subtract, A.mult)
    for k in range(4): column("C%d" % k, "QC", float(k), None, A.is_equal)
    for j, s in enumerate(SHIFT):
        column("LO%d" % j, "C0", 4096.0 + s, -4096.0, A.mult, A.add)
        column("HI%d" % j, "C0", s - 3586.0, 4096.0, A.mult, A.add)
    column("x0", "C3", 0.5, None, A.mult)
    column("HMC", "C2", 8.0, "x0", A.mult, A.add)
    column("x1", "C1", -8.0, None, A.mult)
    column("MB4", "C0", 4.0, "x1", A.mult, A.add)
    column("MB2", "C0", -2.0, "x1", A.mult, A.add)
    column("Q4", "Q3", 4.0, None, A.mult)
    column("LOW", "QC", 1.5, None, A.is_lt)
    column("KEEP", "QC", 1.0, None, A.not_equal)
    column("EVEN", "C0", "C2", None, A.add)
    dif, rel, BD = T.dif[:, :], T.rel[:, :], T.BD[:, :]
    V(c128, ["dif", "Q"], ["rel"], ts(rel, dif, C["Q"], None, A.add))
    V(c128, ["rel"], ["tmp"], ts(T.tmp[:, :], rel, -0.5, None, A.is_gt))
    V(c128, ["rel"], ["BD"], ts(BD, rel, 15.5, None, A.is_lt))
    V(("2", 128), ["tmp", "BD"], ["BD"], tt(BD, BD, T.tmp[:, :], A.mult))
    V(c1, ["dif", "PIDF", "Q"], ["colm"], ts(T.colm[:, :], T.dif[:, 0:16], C["PIDF"], C["Q"], A.add, A.is_equal))
    V(c1, ["colm"], ["cd0"], ts(T.cold[:, 0:4], T.colm[:, 8:12], 16.0, None, A.mult))
    V(c1, ["colm", "cd0"], ["cd"], tt(T.cold[:, 4:8], T.cold[:, 0:4], T.colm[:, 12:16], A.add))
    V(c1, ["colm"], ["cx0"], ts(T.cold[:, 8:12], T.colm[:, 0:4], 16.0, None, A.mult))
    V(c1, ["cd", "cx0"], ["cx"], tt(T.cold[:, 12:16], T.cold[:, 8:12], T.cold[:, 4:8], A.add))
    V(c1, ["colm"], ["cm"], tt(T.cold[:, 16:20], T.colm[:, 0:4], T.colm[:, 4:8], A.add))
    V(c1, ["colm"], ["ck"], ts(T.cold[:, 20:24], T.colm[:, 0:4], 0.0625, None, A.mult))
    V(c1, ["i2", "Q3"], ["cq"], ts(T.cq[:, :], T.i2[:, 0:4], 0.25, C["Q3"], A.mult, A.add))
    M = {}
    for k, nm in enumerate(["I", "KP", "E", "HM", "E0"] + every("RX") + every("RD") + every("MA")):
        M[nm] = T.MH[:, 128 * k:128 * k + 128]
    counts = {s: ["N%d_%d" % (s, p) for p in range(4)] for s in STEPS}
    casts = every("NC")
    single = ["S16", "S8", "S4", "S2", "S1", "SH", "I2", "J2", "U16", "U8", "U4", "U2", "U1", "U0", "BK"]
    for k, nm in enumerate(sum(counts.values(), []) + casts + every("R1") + every("RK") + single):
        M[nm] = T.MB[:, 128 * k:128 * k + 128]
    M["I4"], M["J4"], M["H4"] = T.MF[:, 0:128], T.MF[:, 128:256], T.MF[:, 256:384]
    for p in range(4):
        x = str(p)
        V(c128, ["rel"], [casts[p]], ts(M[casts[p]], rel, float(4 + p), None, A.is_equal))
        V(c128, ["rel"], [counts[8][p]], ts(M[counts[8][p]], rel, float(p), None, A.is_equal))
        for s in (16, 4, 2, 1):
            S(c128, [counts[8][p]], [counts[s][p]], act(M[counts[s][p]], M[counts[8][p]], scale=s / 8.0))
        V(c128, ["BD", "cx"], ["RX" + x], ts(M["RX" + x], BD, col(T.cold, 12 + p), None, A.mult))
        V(c128, ["BD", "cd"], ["RD" + x], ts(M["RD" + x], BD, col(T.cold, 4 + p), None, A.mult))
        S(c128, ["BD", "cm"], ["R1" + x], act(M["R1" + x], BD, scale=col(T.cold, 16 + p)))
        S(c128, ["BD", "ck"], ["RK" + x], act(M["RK" + x], BD, scale=col(T.cold, 20 + p)))
        V(c128, ["rel", "cq", "LOW"], ["MA" + x], ts(M["MA" + x], rel, col(T.cq, p), C["LOW"], A.is_equal, A.mult))
    V(c128, ["dif"], ["I"], ts(M["I"], dif, 0.0, None, A.is_equal))
    V(c128, ["dif"], ["I4"], ts(M["I4"], dif, 0.0, None, A.is_equal))
    if any(c in "BD" for r in SHARE for x in r for c in x["T"] + x["S"]) or any(x["ps"] < 5 for r in SHARE for x in r):
        S(c128, ["I4"], ["J4"], act(M["J4"], M["I4"], scale=-1.0))
    if any(c in "CD" for r in SHARE for x in r for c in x["T"] + x["S"] + x.get("first", "")):
        S(c128, ["I4"], ["H4"], act(M["H4"], M["I4"], scale=0.5))
    S(c128, ["I4"], ["I2"], act(M["I2"], M["I4"]))
    S(c128, ["I4"], ["J2"], act(M["J2"], M["I4"], scale=-1.0))
    V(c128, ["dif", "KEEP"], ["KP"], ts(M["KP"], dif, 0.0, C["KEEP"], A.is_equal, A.mult))
    V(c128, ["dif", "LOW"], ["E"], ts(M["E"], dif, 0.0, C["LOW"], A.is_equal, A.mult))
    V(c128, ["dif", "C0"], ["E0"], ts(M["E0"], dif, 8.0, C["C0"], A.is_equal, A.mult))
    V(("2", 128), ["E", "E0"], ["E"], tt(M["E"], M["E"], M["E0"], A.add))
    V(c128, ["rel", "Q3", "HMC"], ["HM"], ts(M["HM"], rel, C["Q3"], C["HMC"], A.is_equal, A.mult))
    V(c128, ["dif", "C0"], ["S1"], ts(M["S1"], dif, 0.0, C["C0"], A.is_equal, A.mult))
    for s in (16, 8, 4, 2):
        S(c128, ["S1"], ["S%d" % s], act(M["S%d" % s], M["S1"], scale=float(s)))
    V(c128, ["dif", "C1"], ["U0"], ts(M["U0"], dif, 4.0, C["C1"], A.is_equal, A.mult))
    V(c128, ["dif", "C1"], ["BK"], ts(M["BK"], dif, -4.0, C["C1"], A.is_equal, A.mult))
    V(("2", 128), ["BK", "U0"], ["BK"], tt(M["BK"], M["BK"], M["U0"], A.add))
    S(c128, ["BK"], ["BK"], act(M["BK"], M["BK"], scale=-float(SHIFT[4])))
    V(("2", 128), ["S1", "U0"], ["U1"], tt(M["U1"], M["S1"], M["U0"], A.subtract))
    for s in (16, 8, 4, 2):
        S(c128, ["U1"], ["U%d" % s], act(M["U%d" % s], M["U1"], scale=float(s)))
    V(c128, ["dif", "C1"], ["U0"], ts(M["U0"], dif, 8.0, C["C1"], A.is_equal, A.mult))
    S(c128, ["U0"], ["U0"], act(M["U0"], M["U0"], scale=8.0))
    V(("2", 128), ["U1", "U0"], ["U1"], tt(M["U1"], M["U1"], M["U0"], A.add))
    V(c128, ["dif", "C0"], ["SH"], ts(M["SH"], dif, 12.0, C["C0"], A.is_equal, A.mult))
    V(c1, ["i0", "Q4", "EVEN"], ["L0"], ts(T.L0[:, :], T.i0[:, :], C["Q4"], C["EVEN"], A.add, A.mult))
    V(c1, ["i1", "C1"], ["HC"], ts(T.HC[:, :], T.i1[:, :], C["C1"], None, A.mult))
    K = {}

    def fill(nm, ap, value):
        K[nm] = ap
        V(c128, [], [nm], lambda: g.vector.memset(ap, value))
    for k, (nm, value) in enumerate((("DOWN", -BIG), ("UP", BIG))): fill(nm, T.KS[:, 64 * k:64 * k + 64], value)
    V(c1, ["UP", "C0", "C1"], ["UP"], ts(K["UP"], K["UP"], C["C0"], C["C1"], A.mult, A.add))
    fill("ONE", T.ONE[0:1, :], 1.0)

    big, gat, gtt, sm = ("1", CH), ("g", CH), ("t", CH), ("1", 64)

    def chunk(h):
        cnt["h"] = h
        x = str(h)
        at = {}
        for k, nm in enumerate(["ta", "sa", "tb", "sb", "T1", "S1", "gT", "gS", "dS", "w"]): at[nm] = (T["W" + x], k * CH, CH)
        for k, nm in enumerate(["vo", "cr", "t2", "s2", "g2"]): at[nm] = (T["B" + x], k * CH, CH)
        for k, nm in enumerate(["m2", "m3", "mq"]): at[nm] = (T["B" + x], 5 * CH + 64 * k, 64)
        for k, nm in enumerate(["Z", "F", "dl"]): at[nm] = (T["H" + x], 64 * k, 64)
        for k, nm in enumerate(["ia", "ib"]): at[nm] = (T["I" + x], 64 * k, 64)
        for k, nm in enumerate(["of", "og"]): at[nm] = (T["O" + x], 16 * k, 16)
        at["pT"], at["pB"], at["pS"], at["pC"] = (T["P" + x], 0, CH), (T["P" + x], CH, CH), (T["Q" + x], 0, CH), (T["Q" + x], CH, CH)
        at["PP"] = (T["P" + x], 0, 2 * CH)
        at["U0"], at["U1"] = (T.U, 2 * CH * h, CH), (T.U, 2 * CH * h + CH, CH)

        def b(nm, first=0, end=None, by=1):
            t, o, w = at[nm]
            if by == 1: return t[:, o + first:o + (w if end is None else end)]
            return t[:, o + first:o + (w if end is None else end):by]
        return b, (lambda nm: nm + x)

    def spread(h, bank, parts):
        b, n = chunk(h)
        reads = []
        for f, nm, _ in parts: reads += [nm] + every(f)
        PE(reads, [n(bank)], [(b(bank, p, CH, 4), [(M[f + str(p)], t) for f, _, t in parts]) for p in range(4)])

    def cycles(terms): return sum(CH * (4 if x[0][1] == "4" else 1) for x in terms)

    def start(h, regions):
        b, n = chunk(h)
        out = b(regions[0]) if len(regions) == 1 else b("PP")
        wide = CH * len(regions)
        op("P", ("pe", wide), ["ONE"], [n(x) for x in regions],
           lambda: g.tensor.matmul(out, T.ONE[0:1, 0:128], T.ONE[0:1, 0:wide], True, False), group="open")

    def onto(h, region, terms, reads, stop):
        b, n = chunk(h)

        def fn():
            ins = None
            for k, (lhs, rhs) in enumerate(terms): ins = g.tensor.matmul(b(region), M[lhs], rhs, False, stop and k == len(terms) - 1)
            return ins
        op("P", ("pe", cycles(terms)), reads + [x[0] for x in terms], [n(region)], fn, group="stop" if stop else "in")

    def sums(h, region, terms, reads):
        b, n = chunk(h)
        PE(reads + [x[0] for x in terms], [n(region)], [(b(region), [(M[l], r) for l, r in terms])], cycles(terms))

    def offsets(h, both, region, shift=0):
        b, n = chunk(h)
        o = b(region, 128, 144)
        PE([n("Z")] + every("MA"), [n(region)], [(o, [(M["MA%d" % a], b("Z", a, 64, 4)) for a in range(4)])])
        V(sm, [n(region)], [n("of")], ts(b("of"), o, -float(shift), None, A.add))
        if both: V(sm, [n(region)], [n("og")], ts(b("og"), o, 1.0 - shift, None, A.add))

    def new_cast(h, src, terms, reads, region):
        b, n = chunk(h)
        o = b(region, 64, 128)
        PE(reads + ["KP"], [n(region)], [(o, [(M["KP"], src)] + terms)])
        V(sm, [n(region)], [n("Z")], cp(b("Z"), o))

    def vote(h, left, right, s, region, up, more, reads):
        b, n = chunk(h)
        o = b(region, 0, 64)
        x = "S%d" % s
        V(big, [n(left), n(right)], [n("vo")], tt(b("vo"), b(left), b(right), A.is_gt))
        PE([n("vo"), x, up, "UP", "DOWN"] + counts[s] + reads, [n(region)],
           [(o, [(M[up], K["UP"])] + [(M[counts[s][p]], b("vo", p, CH, 4)) for p in range(4)] + [(M[x], K["DOWN"])] + more)])
        step[h] += 1
        return o

    def pair(h, t, tw, sw, tn, sn):
        b, n = chunk(h)
        ta, sa = (("t2", "s2"), ("ta", "sa"))[t]
        S(gat, sn + [n("of")], [n(sa)], act(b(sa), sw.indirect(b("of"))))
        S(gat, tn + [n("of")], [n(ta)], act(b(ta), tw.indirect(b("of"))))
        V(gtt, sn + [n("og"), n(sa)], [n("sb")], tt(b("sb"), sw.indirect(b("og")), b(sa), A.subtract))
        V(gtt, tn + [n("og"), n(ta)], [n("tb")], tt(b("tb"), tw.indirect(b("og")), b(ta), A.subtract))

    def current(h, cw, row):
        b, n = chunk(h)
        S(gat, ["cuT", "colm", n("of")], [n("cr")], act(b("cr"), cw.indirect(b("of")), scale=col(T.colm, row)))

    def carried(h, region):
        b, n = chunk(h)
        new_cast(h, b("Z"), [(M[casts[p]], b("cr", p, CH, 4)) for p in range(4)], [n("Z"), n("cr")] + casts, region)

    def place(h, t, k):
        if k == 0:
            if t == 0: return T.AT[:, :], T.AS[:, :], ["AT"], ["AS"], T.coA, ["coA"]
            return T.aT[:, :], T.aS[:, :], every("aT"), every("aS"), T.coA, ["coA"]
        if k == 1:
            return T.bT[:, :], T.bS[:, :], ["bTx", "bTy"] + every("bT"), ["bSx", "bSy"] + every("bS"), T.coB, ["coBx", "coBy"]
        return T.hT[:, CW * h:CW * h + CW], T.hS[:, CW * h:CW * h + CW], ["hT%d" % h], ["hS%d" % h], T.coH, ["coH"]

    def fetch(h, t, k, j, region):
        b, n = chunk(h)
        tw, sw, tn, sn, _, _ = place(h, t, k)
        offsets(h, False, region, SHIFT[j - 1] if j or k else 0)
        gs = "g2" if t == 0 and j >= ps_of(t, k, h) else "gS"
        S(gat, sn + [n("of")], [n(gs)], act(b(gs), sw.indirect(b("of"))))
        if j == 0 or j in share_of(t, h)["both"]: S(gat, tn + [n("of")], [n("gT")], act(b("gT"), tw.indirect(b("of"))))

    def between(h, t, modes, kk, less, where):
        b, n = chunk(h)
        ta, sa = (("t2", "s2"), ("ta", "sa"))[t]
        wide = "24"[t]
        tr, sr = where
        sides = [(sr, "sb", sa, modes[1], less[1]), (tr, "tb", ta, modes[0], less[0])]
        for r, d, a, mode, (x, xn, xw) in sides:
            if mode in "CD":
                terms = [("H4", b(d)), ("I" + wide, b(a))] + ([("J" + xw, x)] if mode == "D" else [])
                sums(h, r, terms, [n(d), n(a)] + (xn if mode == "D" else []))
        sides = [x for x in sides if x[3] not in "CD"]
        inside = [x[0] for x in sides if x[3] != "V"]
        if inside: start(h, inside)
        for r, d, _, mode, _ in sides:
            gr = "in" if inside else None
            if kk is None: V(big, [n("pC"), n(d)], [n(r)], tt(b(r), b("pC"), b(d), A.mult), gr)
            else: S(big, [n(d)], [n(r)], act(b(r), b(d), scale=kk), gr)
        for r, _, a, mode, (x, xn, xw) in sides:
            if mode == "V": continue
            onto(h, r, [("I" + wide, b(a))] + ([("J" + xw, x)] if mode == "B" else []), [n(a)] + (xn if mode == "B" else []), r == inside[-1])
        for r, _, a, mode, _ in sides:
            if mode == "V": V(big, [n(r), n(a)], [n(r)], tt(b(r), b(r), b(a), A.add))

    def settle(h, t):
        b, n = chunk(h)
        modes = share_of(t, h)["end"]
        none = (None, None, None)
        sr = "pS" if modes[1] == "V" else "pB"
        between(h, t, modes, None, (none, none), ("pT", sr))
        if share_of(t, h)["ps"] == 0: S(big, [n(sr)], [n("S1")], act(b("S1"), b(sr)))
        elif sr != "pS": S(big, [n(sr)], [n("pS")], act(b("pS"), b(sr)))

    def hop(h, t, k):
        b, n = chunk(h)
        share = share_of(t, h)
        tw, sw, tn, sn, co, cn = place(h, t, k)
        a0, a1, b0 = col(co, 0), col(co, 1), col(co, 2)
        pB, pT, pS, dS, gT, gS, w, of = [b(x) for x in ("pB", "pT", "pS", "dS", "gT", "gS", "w", "of")]
        t1, s1 = (b("T1"), [n("T1")], "4"), (b("S1"), [n("S1")], "4")
        first = t == 0 and k == 0
        if first: t1, s1 = (T.HT[:, CW * h:CW * h + CW:4], ["HT"], "2"), (T.HS[:, CW * h:CW * h + CW:4], ["HS"], "2")
        xz = [("RX", n("Z"), b("Z"))]

        def weight(test, x, out):
            if test in share["wv"]: V(big, [n(x)] + cn, [n(out)], ts(b(out), b(x), a1, a0, A.mult, A.add))
            else:
                S(big, [n(x)] + cn, [n(out)], act(b(out), b(x), scale=a1))
                S(big, [n(out)] + cn, [n(out)], act(b(out), b(out), bias=a0))

        for j, s in enumerate(STEPS):
            early = j == 0 and k > 0
            if early:
                spread(h, "pC", xz)
                weight(j, "pC", "w")
            else:
                fetch(h, t, k, j, "pC")
                spread(h, "pB", xz)
                weight(j, "pB", "pB")
            if j >= ps_of(t, k, h):
                gs = ("g2", "gS")[t]
                sums(h, "pS", [("I" + "24"[t], b(gs)), ("J" + s1[2], s1[0])], [n(gs)] + s1[1])
                S(big, [n("pS")] + cn, [n("dS")], act(dS, pS, scale=b0))
            else:
                V(big, [n("gS"), n("pS")], [n("dS")], tt(dS, gS, pS, A.subtract))
                S(big, [n("dS")] + cn, [n("dS")], act(dS, dS, scale=b0))
            if j == 0 and not first and share["ps"]: S(big, [n("pS")], [n("S1")], act(b("S1"), pS))
            if early:
                V(big, [n("gT"), n("pT")], [n("pB")], tt(pB, gT, pT, A.subtract))
                V(big, [n("pB"), n("w")], [n("pB")], tt(pB, pB, w, A.mult))
            else:
                if j == 0 or j in share["both"]: V(big, [n("gT"), n("pT")], [n("gT")], tt(gT, gT, pT, A.subtract))
                else: V(gtt, tn + [n("of")] + t1[1], [n("gT")], tt(gT, tw.indirect(of), t1[0], A.subtract))
                V(big, [n("pB"), n("gT")], [n("pB")], tt(pB, pB, gT, A.mult))
            o = vote(h, "pB", "dS", s, "pC", "U%d" % s, [(M["I"], b("Z"))], [n("Z"), "I"])
            if j == 0 and not first: S(big, [n("pT")], [n("T1")], act(b("T1"), pT))
            V(sm, [n("pC"), "LO%d" % j, "HI%d" % j], [n("Z")], ts(b("Z"), o, C["LO%d" % j], C["HI%d" % j], A.max, A.min))
        offsets(h, True, "pC", SHIFT[4])
        if k == 0: current(h, T.cuT[:, :], 1)
        pair(h, t, tw, sw, tn, sn)
        for j, s in enumerate((4, 2, 1)):
            mt = (None, (n("m2"), b("m2")), (n("m3"), b("m3")))[j]
            modes = share["first"][j] * 2 if first else share["T"][j] + share["S"][j]
            tr, sr = ("pS" if modes[0] == "V" and modes[1] != "V" else "pT"), "pB"
            if j: spread(h, "pC", [("RK",) + mt])
            spread(h, "pS", xz + ([("R1",) + mt] if j else []))
            if tr == "pS" or j == 0: weight(5 + j, "pS", "w")
            if j == 0 and k < 2:
                if k == 0: carried(h, "pC")
                else: new_cast(h, b("Z"), [(M["I"], T.HC[:, :])], [n("Z"), "I", "HC"], "pC")
                fetch(h, t, k + 1, 0, "pC")
            between(h, t, modes, None if j else 0.5, (t1, s1), (tr, sr))
            if tr != "pS" and j: weight(5 + j, "pS", "w")
            if modes[1] in "BD": S(big, [n(sr)] + cn, [n("dS")], act(dS, b(sr), scale=b0))
            else:
                V(big, [n(sr)] + s1[1], [n("dS")], tt(dS, b(sr), s1[0], A.subtract))
                S(big, [n("dS")] + cn, [n("dS")], act(dS, dS, scale=b0))
            if modes[0] not in "BD": V(big, [n(tr)] + t1[1], [n(tr)], tt(b(tr), b(tr), t1[0], A.subtract))
            V(big, [n(tr), n("w")], [n(tr)], tt(b(tr), b(tr), w, A.mult))
            o = vote(h, tr, "dS", s, "pC", "S%d" % s, [(M["S1"], mt[1])] if j else [], [mt[0], "S1"] if j else [])
            nxt, mb = ("m2", "m3", "mq")[j], ("MB4", "MB2", "MB2")[j]
            S(sm, [n("pC"), mb], [n(nxt)], act(b(nxt), o, bias=C[mb]))
        zr = "pB" if k < 2 and share["end"][1] == "V" else "pS"
        o = b(zr, 64, 128)
        spread(h, "pC", [("RK", n("mq"), b("mq"))])
        PE([n("Z"), n("mq"), "E", "SH", "BK", "UP"], [n(zr)], [(o, [(M["E"], b("Z")), (M["SH"], b("mq")), (M["BK"], K["UP"])])])
        V(sm, [n(zr)], [n("Z")], cp(b("Z"), o))
        if k < 2:
            settle(h, t)
            return
        olds = [(tab[:, CW * h + t:CW * h + CW:4], [nm], "2") for tab, nm in ((T.HT, "HT"), (T.HS, "HS"))]
        regions = ("pT", "pB")
        between(h, t, "BB", None, olds, regions)
        for u in (1, 0): S(big, [n(regions[u])], [n(regions[u])], act(b(regions[u]), b(regions[u]), scale=0.25))
        for u in (1, 0):
            r, (old, on, _) = regions[u], olds[u]
            un, uu = n("U%d" % u), b("U%d" % u)
            V(big, [n(r)] + on, [un], tt(uu, b(r), old, A.add))
            if t == 0: S(big, [un], [n(("hT", "hS")[u])], act((T.hT, T.hS)[u][:, CW * h:CW * h + CW:4], uu))
            else: dma("Y", [un], [], (T.yt, T.ys)[u][:, CH * h:CH * h + CH], uu, 1 << 17)

    for h in range(NC):
        b, n = chunk(h)
        S(big, ["HT"], [n("pT")], act(b("pT"), T.HT[:, CW * h:CW * h + CW:4]))
        if ps_of(0, 0, h): S(big, ["HS"], [n("pS")], act(b("pS"), T.HS[:, CW * h:CW * h + CW:4]))
        new_cast(h, T.L0[:, :], [(M[casts[p]], T.cuT[:, CW * h + 4 * p:CW * h + CW:16]) for p in range(4)], ["L0", "cuT"] + casts, "pC")
    dma("Y", ["ccA"], ["cuT"], T.cuT[1:128:16, :], T.ccA[:, :], 65536)
    dma("Y", ["dco"], ["coBx"], T.coB[0:112, 0:3], T.dco[16:128, :], 1536)
    dma("Y", ["dco"], ["coBy"], T.coB[112:128, 0:3], T.dco[0:16, :], 1536)
    for h in range(NC):
        for k in range(3): hop(h, 0, k)
    for h in range(NC):
        send(HA, ["U0%d" % h, "U1%d" % h], ["Lx%d" % h, "Ly%d" % h],
             T.L1[:, 2 * CH * h:2 * CH * (h + 1)], T.U[:, 2 * CH * h:2 * CH * (h + 1)], 1 << 18)
    send(HB, every("U0") + every("U1"), ["dU"], T.dU[:, :], T.U[:, :], 1 << 20)

    def put(h, tabs, names, more, pool):
        chunk(h)
        u = str(h)
        for x in (0, 1):
            out, in_ = tabs[x][:, CW * h:CW * h + CW:4], T.L1[:, (2 * h + x) * CH:(2 * h + x + 1) * CH]
            if pool: op("G", ("n", 170 + 2 * CH * 0.83), ["Lx" + u, "Ly" + u] + more, [names[x] + u], keep(out, in_))
            else: S(big, ["Lx" + u, "Ly" + u] + more, [names[x] + u], act(out, in_))
    for h in range(NC): put(h, (T.aT, T.aS), ("aT", "aS"), [], False)
    dma("Y", ["dU"], every("Lx"), T.L1[0:112, :], T.dU[16:128, :], 7 << 17)
    dma("Y", ["dU"], every("Ly"), T.L1[112:128, :], T.dU[0:16, :], 1 << 17)
    for h in range(NC): put(h, (T.bT, T.bS), ("bT", "bS"), ["bTx", "bTy", "bSx", "bSy"], True)
    for h in range(NC):
        b, n = chunk(h)
        o = b("pC", 0, 64)
        PE([n("Z"), "L0", "HM"], [n("pC")], [(o, [(M["HM"], b("Z")), (M["HM"], T.L0[:, :])])])
        V(sm, [n("pC")], [n("ia")], cp(b("ia"), o))
        V(sm, [n("ia")], [n("ib")], ts(b("ib"), b("ia"), 4, None, A.arith_shift_right))
        V(sm, [n("ib")], [n("dl")], cp(b("dl"), b("ib")))
        V(sm, [n("ia")], [n("ib")], ts(b("ib"), b("ia"), 15, None, A.bitwise_and))
        V(sm, [n("ib")], [n("m2")], cp(b("m2"), b("ib")))
        V(sm, [n("ia")], [n("ia")], ts(b("ia"), b("ia"), 14, None, A.bitwise_and))
        V(sm, [n("ia")], [n("m3")], cp(b("m3"), b("ia")))
        o1, o2 = b("pC", 0, 64), b("pC", 64, 128)
        PE([n("dl"), n("m2"), n("m3"), "E", "SH", "I", "HC"], [n("pC")],
           [(o1, [(M["E"], b("dl")), (M["I"], T.HC[:, :]), (M["SH"], b("m2"))]), (o2, [(M["E"], b("dl")), (M["SH"], b("m3"))])])
        V(sm, [n("pC")], [n("Z")], cp(b("Z"), o1))
        V(sm, [n("pC")], [n("F")], cp(b("F"), o2))
        offsets(h, True, "pC")
        tw, sw, tn, sn, _, _ = place(h, 1, 2)
        pair(h, 1, tw, sw, tn, sn)
        current(h, T.cuT[:, CW * h:CW * h + CW], 0)
        carried(h, "pB" if share_of(1, h)["end"][1] == "V" else "pS")
        spread(h, "pC", [("RK", n("m2"), b("m2"))])
        settle(h, 1)
        step[h] += 1
        for k in range(3): hop(h, 1, k)
        spread(h, "pC", [("RD", n("Z"), b("Z")), ("RD", n("F"), b("F"))])
        S(big, [n("pC")], [n("gS")], act(b("gS"), b("pC"), scale=0.5))
        dma("Y", [n("gS")], [], T.yd[:, CH * h:CH * h + CH], T["W%d" % h][0:128:16, 7 * CH:8 * CH], 8192)
    return ops


def spans(ops, e):
    cost = [cost_ns(o["cost"], e) for o in ops]
    span = [c + (700 + e["dl"] + o["bytes"] / e["bw"] if o["kind"] in ("dma", "send") else 0) for c, o in zip(cost, ops)]
    return cost, span, [list(o["deps"]) + list(o["sim"]) for o in ops]


def arrange(ops, e, order=None, given=None):
    n = len(ops)
    cost, span, pre = spans(ops, e)
    users = [[] for _ in range(n)]
    for i in range(n):
        for d in pre[i]: users[d].append(i)
    prio = given
    if prio is None:
        prio = [0.0] * n
        for i in range(n - 1, -1, -1):
            prio[i] = span[i] + max([prio[u] + e["lat"] for u in users[i]] + [0.0])
        for i in range(n):
            prio[i] += (1e6 if ops[i]["cost"] == ("1", 64) else 0) - 1000 * (ops[i]["step"] + e["lead"] * ops[i]["h"])
    fixed = {q: [i for i in range(n) if ops[i]["eng"] == q] for q in "G"}
    if order is not None:
        for q in "VSPY": fixed[q] = order[q]
    pos = {q: 0 for q in fixed}
    out = {q: [] for q in "VSPGYX"}
    free = {q: 0.0 for q in "VSPGYX"}
    wire = [0.0]
    left = [len(p) for p in pre]
    ready = [0.0] * n
    done = [0.0] * n
    pool = {q: [i for i in range(n) if ops[i]["eng"] == q and left[i] == 0] for q in "VSPGYX"}
    for _ in range(n):
        best = None
        for q in "VSPGYX":
            if q in fixed:
                cand = fixed[q][pos[q]:pos[q] + 1]
                if cand and left[cand[0]]: cand = []
            else: cand = pool[q]
            if not cand: continue
            t0 = max(free[q], min(ready[i] for i in cand))
            if q == "Y": i = min((i for i in cand if ready[i] <= t0))
            else: i = max((i for i in cand if ready[i] <= t0), key=lambda i: (prio[i], -i))
            if best is None or t0 < best[0]: best = (t0, q, i)
        t0, q, i = best
        pool[q].remove(i)
        if q in pos: pos[q] += 1
        out[q].append(i)
        if q != "X": free[q] = t0 + cost[i]
        fin = t0 + cost[i]
        if ops[i]["kind"] in ("dma", "send"):
            wire[0] = max(wire[0], fin + e["dl"]) + ops[i]["bytes"] / e["bw"]
            fin = wire[0] + 700
        done[i] = fin
        for u in users[i]:
            ready[u] = max(ready[u], fin + (0.0 if i in ops[u]["soft"] else e["lat"]))
            left[u] -= 1
            if left[u] == 0: pool[ops[u]["eng"]].append(u)
    return out, max(done), done


def backward(ops, e, done):
    n = len(ops)
    cost, span, pre = spans(ops, e)
    lane = [o["eng"] if o["eng"] in "VSP" else "O" for o in ops]
    left = [0] * n
    for i in range(n):
        for d in pre[i]: left[d] += 1
    free = {q: 0.0 for q in "VSPO"}
    ready = [0.0] * n
    fin = [0.0] * n
    pool = {q: [i for i in range(n) if left[i] == 0 and lane[i] == q] for q in "VSPO"}
    for _ in range(n):
        best = None
        for q in "VSPO":
            if not pool[q]: continue
            t0 = max(free[q], min(ready[i] for i in pool[q]))
            i = max((i for i in pool[q] if ready[i] <= t0), key=lambda i: (done[i], i))
            if best is None or t0 < best[0]: best = (t0, q, i)
        t0, q, i = best
        pool[q].remove(i)
        if q != "O": free[q] = t0 + cost[i]
        fin[i] = t0 + span[i]
        for d in pre[i]:
            ready[d] = max(ready[d], fin[i] + (0.0 if d in ops[i]["soft"] else e["lat"]))
            left[d] -= 1
            if left[d] == 0: pool[lane[d]].append(d)
    return fin


def rank_program(g, core, T, topo):
    if T.rank_of(core) is None:
        return
    ops = plan(g, T, topo, core)
    order, _, done = arrange(ops, EST)
    for _ in range(2): order, _, done = arrange(ops, EST, given=backward(ops, EST, done))
    queue = {"V": g.vector, "S": g.scalar, "P": g.tensor, "G": g, "Y": g.sync}
    token = {}
    for q in "VSPG":
        k = 0
        for i in order[q]:
            if ops[i]["kind"] == "c":
                k += 1
                token[i] = (q, k)
    for i, o in enumerate(ops):
        if o["kind"] != "c": token[i] = (o["sem"], o["val"])
    known = {q: {} for q in queue}
    clock = {}
    at = {q: 0 for q in queue}
    for i in order["X"]: clock[i] = {}
    going = True
    while going:
        going = False
        for q in queue:
            while at[q] < len(order[q]) and all(d in clock for d in ops[order[q][at[q]]]["deps"]):
                i = order[q][at[q]]
                at[q] += 1
                going = True
                kn = known[q]
                for d in sorted(ops[i]["deps"], key=lambda d: -done[d]):
                    s, v = token[d]
                    if kn.get(s, 0) >= v or d in ops[i]["soft"]: continue
                    queue[q].wait_ge(T.sem[s], v)
                    kn[s] = v
                    for s2, v2 in clock[d].items():
                        if kn.get(s2, 0) < v2: kn[s2] = v2
                clock[i] = dict(kn)
                ins = ops[i]["fn"]()
                if ops[i]["kind"] == "c": ins.then_inc(T.sem[q], 1)
                elif ops[i]["kind"] == "dma": ins.then_inc(T.sem[token[i][0]], 16)
    top = {}
    for s, v in token.values(): top[s] = max(top.get(s, 0), v)
    for s, v in top.items():
        if known["G"].get(s, 0) < v: g.wait_ge(T.sem[s], v)
